import numpy as np
import ml_dtypes


def mxq(x, axis, fmt="e4m3"):
    dtype, down = {"e4m3": (ml_dtypes.float8_e4m3fn, 7), "e5m2": (ml_dtypes.float8_e5m2, 14)}[fmt]
    v = np.moveaxis(np.asarray(x, np.float32).astype(ml_dtypes.bfloat16).astype(np.float64), axis, -1)
    blocks = v.reshape(v.shape[:-1] + (-1, 32))
    amax = np.abs(blocks).max(-1, keepdims=True)
    byte = np.maximum(np.where(amax > 0, np.frexp(amax)[1] - 1 + 127, 0) - down, 1)
    scale = np.exp2(byte - 127.0)
    codes = (blocks / scale).astype(np.float32).astype(dtype).astype(np.float64)
    return np.moveaxis((codes * scale).reshape(v.shape), -1, axis)


WIDE = False


def mx_kscale(k):
    if not WIDE:
        return np.ones(k)
    levels = np.array([10, -10, 5, -5, 0])
    if k % 512:
        return np.exp2(np.random.permutation(np.resize(levels, k // 32))).repeat(32)
    a = np.empty((k // 512, 16))
    for p in range(k // 512):
        a[p, :8] = np.random.permutation(np.resize(levels, 8))
        for g in range(8):
            far = levels[np.abs(levels - a[p, g]) >= 10]
            a[p, g + 8] = far[np.random.randint(len(far))]
    return np.exp2(a.ravel()).repeat(32)


def f64(x):
    return np.asarray(x).astype(np.float64)


def striped(idx):
    return np.tile(idx.reshape(-1, 16).T, (8, 1)).astype(np.uint16)


def unstriped(offs):
    return offs[:16].T.reshape(-1).astype(np.int64)


E2M1 = np.array([0.0, 0.5, 1.0, 1.5, 2.0, 3.0, 4.0, 6.0, -0.0, -0.5, -1.0, -1.5, -2.0, -3.0, -4.0, -6.0])


def pack_weight(w, fmt):
    k, n = w.shape
    w = f64(np.asarray(w, np.float32).astype(ml_dtypes.bfloat16)).reshape(k // 32, 32, n)
    amax = np.abs(w).max(1)
    if fmt == "e4m3":
        byte = np.frexp(amax)[1] - 1 + 127 - 7
    else:
        mant, ex = np.frexp(amax / 6.0)
        byte = np.where(mant > 0.5, ex, ex - 1) + 127
    byte = np.clip(np.where(amax > 0, byte, 1), 1, 254)
    scaled = (w * np.exp2(127.0 - byte)[:, None, :]).reshape(k, n).astype(np.float32)
    by_word = np.ascontiguousarray(scaled.reshape(k // 512, 128, 4, n).transpose(0, 1, 3, 2))
    if fmt == "e4m3":
        words = by_word.astype(ml_dtypes.float8_e4m3fn).view(np.uint8)
    else:
        c = by_word.astype(ml_dtypes.float4_e2m1fn).view(np.uint8) & 0xF
        words = (c[..., 0::2] | (c[..., 1::2] << 4)).reshape(k // 512, 128, 2 * n)
    return np.ascontiguousarray(words), np.ascontiguousarray(byte.astype(np.uint8).reshape(k // 512, 16, n))


def unpack_weight(words, scales, fmt):
    g, _, n = scales.shape
    words = np.ascontiguousarray(words).reshape(g, 128, n, -1)
    if fmt == "e4m3":
        vals = words.view(ml_dtypes.float8_e4m3fn).astype(np.float64)
    else:
        nib = np.empty((g, 128, n, 4), np.uint8)
        nib[..., 0::2] = words & 0xF
        nib[..., 1::2] = words >> 4
        vals = E2M1[nib]
    vals = vals * np.repeat(np.exp2(scales.astype(np.float64) - 127.0), 8, axis=1)[..., None]
    return vals.transpose(0, 1, 3, 2).reshape(g * 512, n)


def gelu(v):
    return 0.5 * v * (1.0 + np.tanh(np.sqrt(2.0 / np.pi) * (v + 0.044715 * v**3)))


K, K2, T, S, H, N = 1024, 512, 2048, 1024, 1024, 512

def setup_inputs():
    n = np.random.standard_normal
    s = mx_kscale(K)[:, None]
    s2 = mx_kscale(K2)[:, None]
    u = mx_kscale(H)[:, None]
    tab_words, tab_scales = pack_weight(n((K, T)) * s, "e4m3")
    tab2_words, tab2_scales = pack_weight(n((K2, T)) * s2, "e4m3")
    wp = (0.5 * n((K, H)) / np.sqrt(K) / s).astype(np.float32)
    wb_words, wb_scales = pack_weight(0.5 * n((K2, H)) / np.sqrt(K2) / s2, "e2m1")
    adv = (n((H, S)) * u).astype(np.float32)
    wc = (n((H, N)) / np.sqrt(H) / u).astype(np.float32)
    bc = (0.5 * n(N)).astype(np.float32)
    return {"tab_words": tab_words, "tab_scales": tab_scales,
            "tab2_words": tab2_words, "tab2_scales": tab2_scales,
            "offs": striped(np.random.permutation(T)[:S]),
            "offs2": striped(np.random.permutation(T)[:S]),
            "wp": wp, "wb_words": wb_words, "wb_scales": wb_scales,
            "adv": adv, "wc": wc, "bc": bc}

def reference(tab_words, tab_scales, tab2_words, tab2_scales, offs, offs2, wp, wb_words, wb_scales, adv, wc, bc):
    v = unpack_weight(tab_words, tab_scales, "e4m3")[:, unstriped(offs)]
    v2 = unpack_weight(tab2_words, tab2_scales, "e4m3")[:, unstriped(offs2)]
    wb = unpack_weight(wb_words, wb_scales, "e2m1")
    a = mxq(f64(wp), 0, "e4m3").T @ v
    b = wb.T @ v2
    rho = np.minimum(np.exp(a - b), 2.0)
    z = rho * f64(adv)
    y = mxq(f64(wc), 0, "e4m3").T @ mxq(z, 0, "e4m3")
    return y + f64(bc)[:, None]

@@ -1,0 +1,238 @@
+from contextlib import ExitStack
+
+import concourse.mybir as mybir
+
+K, K2, T, S, H, N = 1024, 512, 2048, 1024, 1024, 512
+FLOPS = 2 * S * (K * H + K2 * H + H * N)
+
+F32 = mybir.dt.float32
+BF16 = mybir.dt.bfloat16
+I32 = mybir.dt.int32
+U32 = mybir.dt.uint32
+U16 = mybir.dt.uint16
+U8 = mybir.dt.uint8
+FP8X4 = mybir.dt.float8_e4m3fn_x4
+FP4X4 = mybir.dt.float4_e2m1fn_x4
+ACT = mybir.ActivationFunctionType
+ALU = mybir.AluOpType
+
+P = 128
+PACK = 4
+PASS = P * PACK
+W = 512
+CLIP = 2.0
+
+
+def tile_list_importance_weighted_critic_kernel(
+    tc, tab_words, tab_scales, tab2_words, tab2_scales, offs, offs2, wp, wb_words, wb_scales, adv, wc, bc, out
+):
+    nc = tc.nc
+    with ExitStack() as ctx:
+        keep = ctx.enter_context(tc.tile_pool(name="keep", bufs=1))
+        stage = ctx.enter_context(tc.tile_pool(name="stage", bufs=3))
+        psum = ctx.enter_context(tc.psum_pool(name="psum", bufs=8))
+
+        def held(name, shape, dtype):
+            return keep.tile(shape, dtype, name=name, align_bytes=64)
+
+        list1 = held("list1", [P, S // 16], U16)
+        list2 = held("list2", [P, S // 16], U16)
+        v_words = [held("v_words%d" % a, [P, T], U32) for a in range(2)]
+        v2_words = held("v2_words", [P, T], U32)
+        v_scales = held("v_scales", [P, T], U8)
+        v2_scales = held("v2_scales", [P, T], U8)
+        wb_raw = held("wb_raw", [P, 2 * H], U8)
+        wb_scales_raw = held("wb_scales_raw", [P, H], U8)
+        bias = held("bias", [P, N // P], F32)
+
+        nc.gpsimd.memset(v2_scales[:].bitcast(I32), 0)
+        nc.vector.memset(wb_scales_raw[:].bitcast(I32), 0)
+        nc.vector.memset(v_scales[:].bitcast(I32), 0)
+
+        def load_words(dst, src, parts):
+            words = src.rearrange("p t i -> p (t i)").bitcast(I32)
+            for part in range(parts):
+                cols = slice(part * T // parts, (part + 1) * T // parts)
+                nc.sync.dma_start(out=dst[:, cols].bitcast(I32), in_=words[:, cols])
+
+        def load_scales(dst, src):
+            passes = src.shape[0]
+            for q in range(4):
+                nc.sync.dma_start(
+                    out=dst[32 * q : 32 * q + 4 * passes, :].bitcast(I32),
+                    in_=src[:, 4 * q : 4 * q + 4, :].bitcast(I32),
+                )
+
+        def load_rows(name, src):
+            raw = held(name, [P, PACK, src.shape[1]], F32)
+            nc.sync.dma_start(out=raw[:], in_=src.rearrange("(p k) c -> p k c", k=PACK))
+            return raw
+
+        def blk(i):
+            return slice(i * 512, (i + 1) * 512)
+
+        wp_raw = {}
+        adv_raw = {}
+        wc_raw = {}
+        nc.sync.dma_start(list2[:], offs2)
+        load_words(v2_words, tab2_words[0], 2)
+        nc.sync.dma_start(out=wb_raw[:].bitcast(I32), in_=wb_words[0].bitcast(I32))
+        load_scales(v2_scales, tab2_scales)
+        wp_raw[0, 0] = load_rows("wp00", wp[blk(0), blk(0)])
+        load_scales(wb_scales_raw, wb_scales)
+        nc.sync.dma_start(list1[:], offs)
+        load_words(v_words[0], tab_words[0], 1)
+        load_scales(v_scales, tab_scales)
+        wp_raw[1, 0] = load_rows("wp10", wp[blk(1), blk(0)])
+        with nc.allow_non_contiguous_dma(reason="one bias value a partition"):
+            nc.sync.dma_start(out=bias[:], in_=bc.rearrange("(c p) -> p c", p=P))
+        wp_raw[0, 1] = load_rows("wp01", wp[blk(0), blk(1)])
+        load_words(v_words[1], tab_words[1], 1)
+        wp_raw[1, 1] = load_rows("wp11", wp[blk(1), blk(1)])
+        adv_raw[0, 0] = load_rows("adv00", adv[blk(0), 0:512])
+        adv_raw[1, 0] = load_rows("adv10", adv[blk(1), 0:512])
+        wc_raw[0] = load_rows("wc0", wc[blk(0), :])
+        wc_raw[1] = load_rows("wc1", wc[blk(1), :])
+        adv_raw[0, 512] = load_rows("adv01", adv[blk(0), 512:1024])
+        adv_raw[1, 512] = load_rows("adv11a", adv[blk(1), 512:768])
+        adv_raw[1, 768] = load_rows("adv11b", adv[blk(1), 768:1024])
+
+        def gather(name, window, offsets, h, dtype):
+            picked = held(name, [P, W], dtype)
+            nc.vector.tensor_copy(picked[:], window[:].indirect(offsets[:, 32 * h : 32 * (h + 1)]))
+            return picked
+
+        def quantize(name, grouped):
+            width = grouped.shape[1] // PACK
+            codes = held(name + "_codes", [P, width], U32)
+            scales = held(name + "_scales", [P, width], U8)
+            nc.vector.quantize_mx(out=codes[:].bitcast(FP8X4), scales=scales[:], in_=grouped[:])
+            return codes, scales
+
+        def cast_wp(a, b, on_vector):
+            grouped = stage.tile([P, PACK * W], BF16, name="grouped", align_bytes=64)
+            dst = grouped[:].rearrange("p (t m k) -> p m k t", t=PACK, k=PACK)
+            src = wp_raw[a, b][:].rearrange("p k (m t) -> p m k t", t=PACK)
+            if on_vector:
+                nc.vector.tensor_scalar(dst, src, -1.0, None, ALU.mult)
+            else:
+                nc.scalar.activation(dst, src, ACT.Copy, scale=-1.0)
+            return grouped
+
+        def cast_wc(b, on_vector):
+            grouped = stage.tile([P, PACK * W], BF16, name="grouped", align_bytes=64)
+            dst = grouped[:].rearrange("p (c i k) -> p c k i", i=4, k=PACK)
+            src = wc_raw[b][:].rearrange("p k (c i) -> p c k i", i=4)
+            if on_vector:
+                nc.vector.tensor_copy(dst, src)
+            else:
+                nc.scalar.activation(dst, src, ACT.Copy)
+            return grouped
+
+        g2s = {}
+        g2w = {}
+        g1s = {}
+        g1w = {}
+        wpq = {}
+        g2w[0] = gather("g2w0", v2_words, list2, 0, U32)
+        g2s[0] = gather("g2s0", v2_scales, list2, 0, U8)
+
+        wb_q = held("wb_q", [P, 2 * H], U8)
+        wb_s = held("wb_s", [P, H], U8)
+        nc.vector.tensor_copy(
+            wb_q[:].bitcast(U16).rearrange("p (b t m) -> p b t m", b=2, t=PACK),
+            wb_raw[:].bitcast(U16).rearrange("p (b m t) -> p b t m", b=2, t=PACK),
+        )
+        nc.vector.tensor_copy(
+            wb_s[:].rearrange("p (b t m) -> p b t m", b=2, t=PACK),
+            wb_scales_raw[:].rearrange("p (b m t) -> p b t m", b=2, t=PACK),
+        )
+        g2w[1] = gather("g2w1", v2_words, list2, 1, U32)
+        g2s[1] = gather("g2s1", v2_scales, list2, 1, U8)
+        wpq[0, 0] = quantize("wp00", cast_wp(0, 0, False))
+        for h in range(2):
+            g1w[0, h] = gather("g1w0%d" % h, v_words[0], list1, h, U32)
+            g1s[h] = gather("g1s%d" % h, v_scales, list1, h, U8)
+        wpq[1, 0] = quantize("wp10", cast_wp(1, 0, False))
+        g1w[1, 0] = gather("g1w10", v_words[1], list1, 0, U32)
+        wpq[0, 1] = quantize("wp01", cast_wp(0, 1, False))
+        g1w[1, 1] = gather("g1w11", v_words[1], list1, 1, U32)
+
+        def first_products(b, h):
+            ratio = held("ratio%d%d" % (b, h), [P, PACK, W], F32)
+            for t in range(PACK):
+                bank = psum.tile([P, W], F32, name="bank")
+                c0 = b * PASS + t * P
+                nc.tensor.matmul_mx(
+                    out=bank[:],
+                    lhsT=wb_q[:, 2 * c0 : 2 * (c0 + P)].bitcast(FP4X4),
+                    lhsT_scale=wb_s[:, c0 : c0 + P],
+                    rhs=g2w[h][:].bitcast(FP8X4),
+                    rhs_scale=g2s[h][:],
+                    start=True,
+                    stop=False,
+                )
+                for a in range(2):
+                    codes, scales = wpq[a, b]
+                    nc.tensor.matmul_mx(
+                        out=bank[:],
+                        lhsT=codes[:, t * P : (t + 1) * P].bitcast(FP8X4),
+                        lhsT_scale=scales[:, t * P : (t + 1) * P],
+                        rhs=g1w[a, h][:].bitcast(FP8X4),
+                        rhs_scale=g1s[h][4 * a : P, :],
+                        start=False,
+                        stop=(a == 1),
+                    )
+                nc.scalar.activation(ratio[:, t, :], bank[:], ACT.Exp, scale=-1.0)
+            return ratio
+
+        def weigh(b, j0, width):
+            grouped = stage.tile([P, PACK * width], BF16, name="z_grouped", align_bytes=64)
+            nc.vector.scalar_tensor_tensor(
+                grouped[:].rearrange("p (j t) -> p j t", t=PACK),
+                ratio[b, j0 // W][:, :, j0 % W : j0 % W + width].rearrange("p t j -> p j t"),
+                CLIP,
+                adv_raw[b, j0][:].rearrange("p t j -> p j t"),
+                ALU.min,
+                ALU.mult,
+            )
+            return quantize("z%d_%d" % (b, j0), grouped)
+
+        def critic(j0, width, z_parts, shared):
+            for n in range(N // P):
+                bank = psum.tile([P, width], F32, name="bank")
+                for b in range(2):
+                    codes, scales, first = z_parts[b]
+                    cols = slice(j0 - first, j0 - first + width)
+                    nc.tensor.matmul_mx(
+                        out=bank[:],
+                        lhsT=wcq[b][0][:, n * P : (n + 1) * P].bitcast(FP8X4),
+                        lhsT_scale=wcq[b][1][:, n * P : (n + 1) * P],
+                        rhs=codes[:, cols].bitcast(FP8X4),
+                        rhs_scale=scales[:, cols],
+                        start=(b == 0),
+                        stop=(b == 1),
+                    )
+                result = held("result%d_%d" % (j0, n), [P, width], F32)
+                if shared and n % 2 == 1:
+                    nc.vector.tensor_scalar(result[:], bank[:], bias[:, n : n + 1], None, ALU.add)
+                else:
+                    nc.scalar.activation(result[:], bank[:], ACT.Identity, bias=bias[:, n : n + 1])
+                nc.sync.dma_start(out=out[n * P : (n + 1) * P, j0 : j0 + width], in_=result[:])
+
+        ratio = {}
+        wcq = {}
+        ratio[0, 0] = first_products(0, 0)
+        wpq[1, 1] = quantize("wp11", cast_wp(1, 1, True))
+        ratio[0, 1] = first_products(0, 1)
+        ratio[1, 0] = first_products(1, 0)
+        z00 = weigh(0, 0, 512) + (0,)
+        z10 = weigh(1, 0, 512) + (0,)
+        wcq[0] = quantize("wc0", cast_wc(0, False))
+        wcq[1] = quantize("wc1", cast_wc(1, False))
+        ratio[1, 1] = first_products(1, 1)
+        critic(0, 512, (z00, z10), False)
+        z01 = weigh(0, 512, 512) + (512,)
+        for j0 in (512, 768):
+            z11 = weigh(1, j0, 256) + (j0,)
+            critic(j0, 256, (z01, z11), True)

@@ -186,14 +186,15 @@ def tile_list_importance_weighted_critic_kernel(
                 nc.scalar.activation(ratio[:, t, :], bank[:], ACT.Exp, scale=-1.0)
             return ratio
 
+        def clip(b, h):
+            nc.vector.tensor_scalar(ratio[b, h][:], ratio[b, h][:], CLIP, None, ALU.min)
+
         def weigh(b, j0, width):
             grouped = stage.tile([P, PACK * width], BF16, name="z_grouped", align_bytes=64)
-            nc.vector.scalar_tensor_tensor(
-                grouped[:].rearrange("p (j t) -> p j t", t=PACK),
-                ratio[b, j0 // W][:, :, j0 % W : j0 % W + width].rearrange("p t j -> p j t"),
-                CLIP,
-                adv_raw[b, j0][:].rearrange("p t j -> p j t"),
-                ALU.min,
+            nc.vector.tensor_tensor(
+                grouped[:].rearrange("p (c i t) -> p c t i", i=4, t=PACK),
+                ratio[b, j0 // W][:, :, j0 % W : j0 % W + width].rearrange("p t (c i) -> p c t i", i=4),
+                adv_raw[b, j0][:].rearrange("p t (c i) -> p c t i", i=4),
                 ALU.mult,
             )
             return quantize("z%d_%d" % (b, j0), grouped)
@@ -224,15 +225,19 @@ def tile_list_importance_weighted_critic_kernel(
         wcq = {}
         ratio[0, 0] = first_products(0, 0)
         wpq[1, 1] = quantize("wp11", cast_wp(1, 1, True))
+        clip(0, 0)
         ratio[0, 1] = first_products(0, 1)
         ratio[1, 0] = first_products(1, 0)
         z00 = weigh(0, 0, 512) + (0,)
+        clip(1, 0)
         z10 = weigh(1, 0, 512) + (0,)
         wcq[0] = quantize("wc0", cast_wc(0, False))
         wcq[1] = quantize("wc1", cast_wc(1, False))
         ratio[1, 1] = first_products(1, 1)
+        clip(0, 1)
         critic(0, 512, (z00, z10), False)
         z01 = weigh(0, 512, 512) + (512,)
+        clip(1, 1)
         for j0 in (512, 768):
             z11 = weigh(1, j0, 256) + (j0,)
             critic(j0, 256, (z01, z11), True)

@@ -78,24 +78,25 @@ def tile_list_importance_weighted_critic_kernel(
         load_words(v2_words, tab2_words[0], 2)
         nc.sync.dma_start(out=wb_raw[:].bitcast(I32), in_=wb_words[0].bitcast(I32))
         load_scales(v2_scales, tab2_scales)
-        wp_raw[0, 0] = load_rows("wp00", wp[blk(0), blk(0)])
+        load_words(v_words[0], tab_words[0], 1)
         load_scales(wb_scales_raw, wb_scales)
         nc.sync.dma_start(list1[:], offs)
-        load_words(v_words[0], tab_words[0], 1)
+        wp_rows0 = load_rows("wp0", wp[blk(0), :])
+        wp_raw[0, 0] = wp_rows0[:, :, blk(0)]
+        wp_raw[0, 1] = wp_rows0[:, :, blk(1)]
         load_scales(v_scales, tab_scales)
-        wp_raw[1, 0] = load_rows("wp10", wp[blk(1), blk(0)])
-        with nc.allow_non_contiguous_dma(reason="one bias value a partition"):
-            nc.sync.dma_start(out=bias[:], in_=bc.rearrange("(c p) -> p c", p=P))
-        wp_raw[0, 1] = load_rows("wp01", wp[blk(0), blk(1)])
+        wp_raw[1, 0] = load_rows("wp10", wp[blk(1), blk(0)])[:]
         load_words(v_words[1], tab_words[1], 1)
-        wp_raw[1, 1] = load_rows("wp11", wp[blk(1), blk(1)])
-        adv_raw[0, 0] = load_rows("adv00", adv[blk(0), 0:512])
-        adv_raw[1, 0] = load_rows("adv10", adv[blk(1), 0:512])
+        wp_raw[1, 1] = load_rows("wp11", wp[blk(1), blk(1)])[:]
+        adv_rows0 = load_rows("adv0", adv[blk(0), :])
+        adv_raw[0, 0] = adv_rows0[:, :, blk(0)]
+        adv_raw[0, 1] = adv_rows0[:, :, blk(1)]
+        adv_raw[1, 0] = load_rows("adv10", adv[blk(1), blk(0)])[:]
         wc_raw[0] = load_rows("wc0", wc[blk(0), :])
         wc_raw[1] = load_rows("wc1", wc[blk(1), :])
-        adv_raw[0, 512] = load_rows("adv01", adv[blk(0), 512:1024])
-        adv_raw[1, 512] = load_rows("adv11a", adv[blk(1), 512:768])
-        adv_raw[1, 768] = load_rows("adv11b", adv[blk(1), 768:1024])
+        adv_raw[1, 1] = load_rows("adv11", adv[blk(1), blk(1)])[:]
+        with nc.allow_non_contiguous_dma(reason="one bias value a partition"):
+            nc.sync.dma_start(out=bias[:], in_=bc.rearrange("(c p) -> p c", p=P))
 
         def gather(name, window, offsets, h, dtype):
             picked = held(name, [P, W], dtype)
@@ -112,7 +113,7 @@ def tile_list_importance_weighted_critic_kernel(
         def cast_wp(a, b, on_vector):
             grouped = stage.tile([P, PACK * W], BF16, name="grouped", align_bytes=64)
             dst = grouped[:].rearrange("p (t m k) -> p m k t", t=PACK, k=PACK)
-            src = wp_raw[a, b][:].rearrange("p k (m t) -> p m k t", t=PACK)
+            src = wp_raw[a, b].rearrange("p k (m t) -> p m k t", t=PACK)
             if on_vector:
                 nc.vector.tensor_scalar(dst, src, -1.0, None, ALU.mult)
             else:
@@ -149,14 +150,14 @@ def tile_list_importance_weighted_critic_kernel(
         )
         g2w[1] = gather("g2w1", v2_words, list2, 1, U32)
         g2s[1] = gather("g2s1", v2_scales, list2, 1, U8)
-        wpq[0, 0] = quantize("wp00", cast_wp(0, 0, False))
         for h in range(2):
             g1w[0, h] = gather("g1w0%d" % h, v_words[0], list1, h, U32)
             g1s[h] = gather("g1s%d" % h, v_scales, list1, h, U8)
+        wpq[0, 0] = quantize("wp00", cast_wp(0, 0, False))
         wpq[1, 0] = quantize("wp10", cast_wp(1, 0, False))
         g1w[1, 0] = gather("g1w10", v_words[1], list1, 0, U32)
-        wpq[0, 1] = quantize("wp01", cast_wp(0, 1, False))
         g1w[1, 1] = gather("g1w11", v_words[1], list1, 1, U32)
+        wpq[0, 1] = quantize("wp01", cast_wp(0, 1, False))
 
         def first_products(b, h):
             ratio = held("ratio%d%d" % (b, h), [P, PACK, W], F32)
@@ -192,9 +193,9 @@ def tile_list_importance_weighted_critic_kernel(
         def weigh(b, j0, width):
             grouped = stage.tile([P, PACK * width], BF16, name="z_grouped", align_bytes=64)
             nc.vector.tensor_tensor(
-                grouped[:].rearrange("p (c i t) -> p c t i", i=4, t=PACK),
-                ratio[b, j0 // W][:, :, j0 % W : j0 % W + width].rearrange("p t (c i) -> p c t i", i=4),
-                adv_raw[b, j0][:].rearrange("p t (c i) -> p c t i", i=4),
+                grouped[:].rearrange("p (c i t) -> p c t i", i=2, t=PACK),
+                ratio[b, j0 // W][:, :, j0 % W : j0 % W + width].rearrange("p t (c i) -> p c t i", i=2),
+                adv_raw[b, j0 // W][:, :, j0 % W : j0 % W + width].rearrange("p t (c i) -> p c t i", i=2),
                 ALU.mult,
             )
             return quantize("z%d_%d" % (b, j0), grouped)
@@ -225,17 +226,17 @@ def tile_list_importance_weighted_critic_kernel(
         wcq = {}
         ratio[0, 0] = first_products(0, 0)
         wpq[1, 1] = quantize("wp11", cast_wp(1, 1, True))
-        clip(0, 0)
         ratio[0, 1] = first_products(0, 1)
+        clip(0, 0)
         ratio[1, 0] = first_products(1, 0)
+        ratio[1, 1] = first_products(1, 1)
         z00 = weigh(0, 0, 512) + (0,)
         clip(1, 0)
         z10 = weigh(1, 0, 512) + (0,)
         wcq[0] = quantize("wc0", cast_wc(0, False))
         wcq[1] = quantize("wc1", cast_wc(1, False))
-        ratio[1, 1] = first_products(1, 1)
-        clip(0, 1)
         critic(0, 512, (z00, z10), False)
+        clip(0, 1)
         z01 = weigh(0, 512, 512) + (512,)
         clip(1, 1)
         for j0 in (512, 768):

@@ -19,7 +19,8 @@ ALU = mybir.AluOpType
 P = 128
 PACK = 4
 PASS = P * PACK
-W = 512
+HALF = 512
+UNIT = 256
 CLIP = 2.0
 
 
@@ -29,8 +30,7 @@ def tile_list_importance_weighted_critic_kernel(
     nc = tc.nc
     with ExitStack() as ctx:
         keep = ctx.enter_context(tc.tile_pool(name="keep", bufs=1))
-        stage = ctx.enter_context(tc.tile_pool(name="stage", bufs=3))
-        psum = ctx.enter_context(tc.psum_pool(name="psum", bufs=8))
+        psum = ctx.enter_context(tc.psum_pool(name="psum", bufs=1))
 
         def held(name, shape, dtype):
             return keep.tile(shape, dtype, name=name, align_bytes=64)
@@ -44,22 +44,18 @@ def tile_list_importance_weighted_critic_kernel(
         wb_raw = held("wb_raw", [P, 2 * H], U8)
         wb_scales_raw = held("wb_scales_raw", [P, H], U8)
         bias = held("bias", [P, N // P], F32)
+        banks = [psum.tile([P, HALF], F32, name="bank%d" % i) for i in range(8)]
+        rounded = [held("rounded%d" % i, [P, PACK * HALF], BF16) for i in range(4)]
+        ratio = {(b, h): held("ratio%d%d" % (b, h), [P, PACK, HALF], F32) for b in range(2) for h in range(2)}
 
-        nc.gpsimd.memset(v2_scales[:].bitcast(I32), 0)
-        nc.vector.memset(wb_scales_raw[:].bitcast(I32), 0)
-        nc.vector.memset(v_scales[:].bitcast(I32), 0)
+        def load_words(dst, src):
+            nc.sync.dma_start(out=dst[:].bitcast(I32), in_=src.rearrange("p t i -> p (t i)").bitcast(I32))
 
-        def load_words(dst, src, parts):
-            words = src.rearrange("p t i -> p (t i)").bitcast(I32)
-            for part in range(parts):
-                cols = slice(part * T // parts, (part + 1) * T // parts)
-                nc.sync.dma_start(out=dst[:, cols].bitcast(I32), in_=words[:, cols])
-
-        def load_scales(dst, src):
+        def load_scales(dst, src, first):
             passes = src.shape[0]
-            for q in range(4):
+            for q in (0, 2, 1, 3):
                 nc.sync.dma_start(
-                    out=dst[32 * q : 32 * q + 4 * passes, :].bitcast(I32),
+                    out=dst[32 * q + first : 32 * q + first + 4 * passes, :].bitcast(I32),
                     in_=src[:, 4 * q : 4 * q + 4, :].bitcast(I32),
                 )
 
@@ -69,176 +65,226 @@ def tile_list_importance_weighted_critic_kernel(
             return raw
 
         def blk(i):
-            return slice(i * 512, (i + 1) * 512)
+            return slice(i * PASS, (i + 1) * PASS)
 
         wp_raw = {}
         adv_raw = {}
         wc_raw = {}
+
+        def load_wp(a, b0, count):
+            raw = load_rows("wp%d%d" % (a, b0), wp[blk(a), b0 * PASS : (b0 + count) * PASS])
+            for b in range(count):
+                wp_raw[a, b0 + b] = raw[:, :, blk(b)]
+
+        def load_adv(b, j0, width):
+            raw = load_rows("adv%d_%d" % (b, j0), adv[blk(b), j0 : j0 + width])
+            for j in range(j0, j0 + width, UNIT):
+                adv_raw[b, j // UNIT] = (raw, j0)
+
+        nc.gpsimd.memset(v2_scales[:].bitcast(I32), 0)
+        nc.vector.memset(v_scales[:].bitcast(I32), 0)
+        nc.vector.memset(wb_scales_raw[:].bitcast(I32), 0)
+
         nc.sync.dma_start(list2[:], offs2)
-        load_words(v2_words, tab2_words[0], 2)
-        nc.sync.dma_start(out=wb_raw[:].bitcast(I32), in_=wb_words[0].bitcast(I32))
-        load_scales(v2_scales, tab2_scales)
-        load_words(v_words[0], tab_words[0], 1)
-        load_scales(wb_scales_raw, wb_scales)
+        load_words(v2_words, tab2_words[0])
         nc.sync.dma_start(list1[:], offs)
-        wp_rows0 = load_rows("wp0", wp[blk(0), :])
-        wp_raw[0, 0] = wp_rows0[:, :, blk(0)]
-        wp_raw[0, 1] = wp_rows0[:, :, blk(1)]
-        load_scales(v_scales, tab_scales)
-        wp_raw[1, 0] = load_rows("wp10", wp[blk(1), blk(0)])[:]
-        load_words(v_words[1], tab_words[1], 1)
-        wp_raw[1, 1] = load_rows("wp11", wp[blk(1), blk(1)])[:]
-        adv_rows0 = load_rows("adv0", adv[blk(0), :])
-        adv_raw[0, 0] = adv_rows0[:, :, blk(0)]
-        adv_raw[0, 1] = adv_rows0[:, :, blk(1)]
-        adv_raw[1, 0] = load_rows("adv10", adv[blk(1), blk(0)])[:]
+        nc.sync.dma_start(out=wb_raw[:].bitcast(I32), in_=wb_words[0].bitcast(I32))
+        load_scales(v2_scales, tab2_scales, 0)
+        load_scales(v_scales, tab_scales, 4)
+        load_wp(0, 0, 2)
+        load_scales(wb_scales_raw, wb_scales, 0)
+        load_words(v_words[0], tab_words[0])
+        load_wp(1, 0, 2)
+        load_words(v_words[1], tab_words[1])
+        load_adv(0, 0, HALF)
+        load_adv(1, 0, HALF)
         wc_raw[0] = load_rows("wc0", wc[blk(0), :])
         wc_raw[1] = load_rows("wc1", wc[blk(1), :])
-        adv_raw[1, 1] = load_rows("adv11", adv[blk(1), blk(1)])[:]
+        load_adv(0, HALF, HALF)
         with nc.allow_non_contiguous_dma(reason="one bias value a partition"):
             nc.sync.dma_start(out=bias[:], in_=bc.rearrange("(c p) -> p c", p=P))
+        load_adv(1, HALF, UNIT)
+        load_adv(1, HALF + UNIT, UNIT)
 
-        def gather(name, window, offsets, h, dtype):
-            picked = held(name, [P, W], dtype)
-            nc.vector.tensor_copy(picked[:], window[:].indirect(offsets[:, 32 * h : 32 * (h + 1)]))
+        def gather(name, window, offsets, j0, width, dtype):
+            picked = held(name, [P, width], dtype)
+            nc.vector.tensor_copy(picked[:], window[:].indirect(offsets[:, j0 // 16 : (j0 + width) // 16]))
             return picked
 
         def quantize(name, grouped):
             width = grouped.shape[1] // PACK
             codes = held(name + "_codes", [P, width], U32)
             scales = held(name + "_scales", [P, width], U8)
-            nc.vector.quantize_mx(out=codes[:].bitcast(FP8X4), scales=scales[:], in_=grouped[:])
-            return codes, scales
+            nc.vector.quantize_mx(out=codes[:].bitcast(FP8X4), scales=scales[:], in_=grouped)
+            return [(codes[:, c : c + P], scales[:, c : c + P]) for c in range(0, width, P)]
 
-        def cast_wp(a, b, on_vector):
-            grouped = stage.tile([P, PACK * W], BF16, name="grouped", align_bytes=64)
-            dst = grouped[:].rearrange("p (t m k) -> p m k t", t=PACK, k=PACK)
-            src = wp_raw[a, b].rearrange("p k (m t) -> p m k t", t=PACK)
+        def round_wp(a, b, t0, count, buffer, on_vector):
+            grouped = buffer[:, t0 * PASS : (t0 + count) * PASS]
+            dst = grouped.rearrange("p (t m k) -> p m k t", t=count, k=PACK)
+            src = wp_raw[a, b].rearrange("p k (m t) -> p m k t", t=PACK)[:, :, :, t0 : t0 + count]
             if on_vector:
                 nc.vector.tensor_scalar(dst, src, -1.0, None, ALU.mult)
             else:
                 nc.scalar.activation(dst, src, ACT.Copy, scale=-1.0)
-            return grouped
+            for t, operand in enumerate(quantize("wp%d%d%d" % (a, b, t0), grouped)):
+                wpq[a, b, t0 + t] = operand
 
-        def cast_wc(b, on_vector):
-            grouped = stage.tile([P, PACK * W], BF16, name="grouped", align_bytes=64)
-            dst = grouped[:].rearrange("p (c i k) -> p c k i", i=4, k=PACK)
-            src = wc_raw[b][:].rearrange("p k (c i) -> p c k i", i=4)
+        def round_wc(b, n0, count, buffer, on_vector):
+            grouped = buffer[:, n0 * PASS : (n0 + count) * PASS]
+            dst = grouped.rearrange("p (c i k) -> p c k i", i=4, k=PACK)
+            src = wc_raw[b][:, :, n0 * P : (n0 + count) * P].rearrange("p k (c i) -> p c k i", i=4)
             if on_vector:
                 nc.vector.tensor_copy(dst, src)
             else:
                 nc.scalar.activation(dst, src, ACT.Copy)
-            return grouped
+            for n, operand in enumerate(quantize("wc%d%d" % (b, n0), grouped)):
+                wcq[b, n0 + n] = operand
 
-        g2s = {}
-        g2w = {}
-        g1s = {}
-        g1w = {}
         wpq = {}
-        g2w[0] = gather("g2w0", v2_words, list2, 0, U32)
-        g2s[0] = gather("g2s0", v2_scales, list2, 0, U8)
+        wcq = {}
+        g1w = {}
+
+        def gather_v(a, j0, width):
+            picked = gather("g1w%d_%d" % (a, j0), v_words[a], list1, j0, width, U32)
+            for j in range(j0, j0 + width, UNIT):
+                g1w[a, j // UNIT] = picked[:, j - j0 : j - j0 + UNIT]
 
         wb_q = held("wb_q", [P, 2 * H], U8)
         wb_s = held("wb_s", [P, H], U8)
-        nc.vector.tensor_copy(
-            wb_q[:].bitcast(U16).rearrange("p (b t m) -> p b t m", b=2, t=PACK),
-            wb_raw[:].bitcast(U16).rearrange("p (b m t) -> p b t m", b=2, t=PACK),
-        )
-        nc.vector.tensor_copy(
-            wb_s[:].rearrange("p (b t m) -> p b t m", b=2, t=PACK),
-            wb_scales_raw[:].rearrange("p (b m t) -> p b t m", b=2, t=PACK),
-        )
-        g2w[1] = gather("g2w1", v2_words, list2, 1, U32)
-        g2s[1] = gather("g2s1", v2_scales, list2, 1, U8)
-        for h in range(2):
-            g1w[0, h] = gather("g1w0%d" % h, v_words[0], list1, h, U32)
-            g1s[h] = gather("g1s%d" % h, v_scales, list1, h, U8)
-        wpq[0, 0] = quantize("wp00", cast_wp(0, 0, False))
-        wpq[1, 0] = quantize("wp10", cast_wp(1, 0, False))
-        g1w[1, 0] = gather("g1w10", v_words[1], list1, 0, U32)
-        g1w[1, 1] = gather("g1w11", v_words[1], list1, 1, U32)
-        wpq[0, 1] = quantize("wp01", cast_wp(0, 1, False))
 
-        def first_products(b, h):
-            ratio = held("ratio%d%d" % (b, h), [P, PACK, W], F32)
-            for t in range(PACK):
-                bank = psum.tile([P, W], F32, name="bank")
-                c0 = b * PASS + t * P
-                nc.tensor.matmul_mx(
-                    out=bank[:],
-                    lhsT=wb_q[:, 2 * c0 : 2 * (c0 + P)].bitcast(FP4X4),
-                    lhsT_scale=wb_s[:, c0 : c0 + P],
-                    rhs=g2w[h][:].bitcast(FP8X4),
-                    rhs_scale=g2s[h][:],
-                    start=True,
-                    stop=False,
-                )
-                for a in range(2):
-                    codes, scales = wpq[a, b]
+        def deal(dst, src):
+            nc.vector.tensor_copy(
+                dst.rearrange("p (b t m) -> p b t m", b=2, t=PACK), src.rearrange("p (b m t) -> p b t m", b=2, t=PACK)
+            )
+
+        g2w = gather("g2w", v2_words, list2, 0, S, U32)
+        deal(wb_q[:].bitcast(U16), wb_raw[:].bitcast(U16))
+        g2s = gather("g2s", v2_scales, list2, 0, S, U8)
+        g1s = gather("g1s", v_scales, list1, 0, S, U8)
+        deal(wb_s[:], wb_scales_raw[:])
+        round_wp(0, 0, 0, PACK, rounded[0], False)
+        round_wp(0, 1, 0, PACK, rounded[1], False)
+        gather_v(0, 0, S)
+        for b in range(2):
+            round_wp(1, b, 0, 2, rounded[2 + b], False)
+            round_wp(1, b, 2, 2, rounded[2 + b], True)
+        gather_v(1, 0, UNIT)
+        gather_v(1, UNIT, UNIT)
+        gather_v(1, HALF, HALF)
+
+        def first_products(b, q, first_bank):
+            cols = slice(q * UNIT, (q + 1) * UNIT)
+            j0 = q % 2 * UNIT
+            for u in range(2):
+                bank = banks[first_bank + u]
+                for e in range(2):
+                    c0 = b * PASS + (2 * u + e) * P
                     nc.tensor.matmul_mx(
-                        out=bank[:],
-                        lhsT=codes[:, t * P : (t + 1) * P].bitcast(FP8X4),
-                        lhsT_scale=scales[:, t * P : (t + 1) * P],
-                        rhs=g1w[a, h][:].bitcast(FP8X4),
-                        rhs_scale=g1s[h][4 * a : P, :],
-                        start=False,
-                        stop=(a == 1),
+                        out=bank[:, e * UNIT : (e + 1) * UNIT],
+                        lhsT=wb_q[:, 2 * c0 : 2 * (c0 + P)].bitcast(FP4X4),
+                        lhsT_scale=wb_s[:, c0 : c0 + P],
+                        rhs=g2w[:, cols].bitcast(FP8X4),
+                        rhs_scale=g2s[:, cols],
+                        start=(e == 0),
+                        stop=False,
                     )
-                nc.scalar.activation(ratio[:, t, :], bank[:], ACT.Exp, scale=-1.0)
-            return ratio
+                for a in range(2):
+                    for e in range(2):
+                        codes, scales = wpq[a, b, 2 * u + e]
+                        nc.tensor.matmul_mx(
+                            out=bank[:, e * UNIT : (e + 1) * UNIT],
+                            lhsT=codes.bitcast(FP8X4),
+                            lhsT_scale=scales,
+                            rhs=g1w[a, q].bitcast(FP8X4),
+                            rhs_scale=g1s[4 + 4 * a : P, cols],
+                            start=False,
+                            stop=(a == 1 and e == 1),
+                        )
+                target = ratio[b, q // 2][:, 2 * u : 2 * u + 2, j0 : j0 + UNIT]
+                nc.scalar.activation(target, bank[:].rearrange("p (e j) -> p e j", e=2), ACT.Exp, scale=-1.0)
 
-        def clip(b, h):
-            nc.vector.tensor_scalar(ratio[b, h][:], ratio[b, h][:], CLIP, None, ALU.min)
+        z_codes = {}
+        z_scales = {}
+        for b in range(2):
+            for h in range(2):
+                z_codes[b, h] = held("z_codes%d%d" % (b, h), [P, HALF], U32)
+                z_scales[b, h] = held("z_scales%d%d" % (b, h), [P, HALF], U8)
 
-        def weigh(b, j0, width):
-            grouped = stage.tile([P, PACK * width], BF16, name="z_grouped", align_bytes=64)
+        def clip(b, j0, width):
+            h, first = divmod(j0, HALF)
+            part = ratio[b, h][:, :, first : first + width]
+            nc.vector.tensor_scalar(part, part, CLIP, None, ALU.min)
+
+        def weigh(b, j0, width, buffer):
+            h, first = divmod(j0, HALF)
+            raw, start = adv_raw[b, j0 // UNIT]
+            grouped = buffer[:, PACK * first : PACK * (first + width)]
             nc.vector.tensor_tensor(
-                grouped[:].rearrange("p (c i t) -> p c t i", i=2, t=PACK),
-                ratio[b, j0 // W][:, :, j0 % W : j0 % W + width].rearrange("p t (c i) -> p c t i", i=2),
-                adv_raw[b, j0 // W][:, :, j0 % W : j0 % W + width].rearrange("p t (c i) -> p c t i", i=2),
+                grouped.rearrange("p (c i t) -> p c t i", i=2, t=PACK),
+                ratio[b, h][:, :, first : first + width].rearrange("p t (c i) -> p c t i", i=2),
+                raw[:, :, j0 - start : j0 - start + width].rearrange("p t (c i) -> p c t i", i=2),
                 ALU.mult,
             )
-            return quantize("z%d_%d" % (b, j0), grouped)
+            cols = slice(first, first + width)
+            nc.vector.quantize_mx(out=z_codes[b, h][:, cols].bitcast(FP8X4), scales=z_scales[b, h][:, cols], in_=grouped)
 
-        def critic(j0, width, z_parts, shared):
-            for n in range(N // P):
-                bank = psum.tile([P, width], F32, name="bank")
-                for b in range(2):
-                    codes, scales, first = z_parts[b]
-                    cols = slice(j0 - first, j0 - first + width)
-                    nc.tensor.matmul_mx(
-                        out=bank[:],
-                        lhsT=wcq[b][0][:, n * P : (n + 1) * P].bitcast(FP8X4),
-                        lhsT_scale=wcq[b][1][:, n * P : (n + 1) * P],
-                        rhs=codes[:, cols].bitcast(FP8X4),
-                        rhs_scale=scales[:, cols],
-                        start=(b == 0),
-                        stop=(b == 1),
-                    )
-                result = held("result%d_%d" % (j0, n), [P, width], F32)
-                if shared and n % 2 == 1:
-                    nc.vector.tensor_scalar(result[:], bank[:], bias[:, n : n + 1], None, ALU.add)
+        def critic_pass(target, b, n, j0, width, start, stop):
+            codes, scales = wcq[b, n]
+            cols = slice(j0 % HALF, j0 % HALF + width)
+            nc.tensor.matmul_mx(
+                out=target,
+                lhsT=codes.bitcast(FP8X4),
+                lhsT_scale=scales,
+                rhs=z_codes[b, j0 // HALF][:, cols].bitcast(FP8X4),
+                rhs_scale=z_scales[b, j0 // HALF][:, cols],
+                start=start,
+                stop=stop,
+            )
+
+        def critic(bank, n0, count, j0, width, on_vector):
+            for b in range(2):
+                for e in range(count):
+                    target = bank[:, e * width : (e + 1) * width]
+                    critic_pass(target, b, n0 + e, j0, width, b == 0 and e == 0, b == 1 and e == count - 1)
+            result = held("result%d_%d" % (j0, n0), [P, count, width], F32)
+            for e in range(count):
+                source = bank[:, e * width : (e + 1) * width]
+                column = bias[:, n0 + e : n0 + e + 1]
+                if on_vector:
+                    nc.vector.tensor_scalar(result[:, e, :], source, column, None, ALU.add)
                 else:
-                    nc.scalar.activation(result[:], bank[:], ACT.Identity, bias=bias[:, n : n + 1])
-                nc.sync.dma_start(out=out[n * P : (n + 1) * P, j0 : j0 + width], in_=result[:])
+                    nc.scalar.activation(result[:, e, :], source, ACT.Identity, bias=column)
+            rows = out[n0 * P : (n0 + count) * P, j0 : j0 + width]
+            nc.sync.dma_start(out=rows.rearrange("(e p) j -> p e j", p=P), in_=result[:])
 
-        ratio = {}
-        wcq = {}
-        ratio[0, 0] = first_products(0, 0)
-        wpq[1, 1] = quantize("wp11", cast_wp(1, 1, True))
-        ratio[0, 1] = first_products(0, 1)
-        clip(0, 0)
-        ratio[1, 0] = first_products(1, 0)
-        ratio[1, 1] = first_products(1, 1)
-        z00 = weigh(0, 0, 512) + (0,)
-        clip(1, 0)
-        z10 = weigh(1, 0, 512) + (0,)
-        wcq[0] = quantize("wc0", cast_wc(0, False))
-        wcq[1] = quantize("wc1", cast_wc(1, False))
-        critic(0, 512, (z00, z10), False)
-        clip(0, 1)
-        z01 = weigh(0, 512, 512) + (512,)
-        clip(1, 1)
-        for j0 in (512, 768):
-            z11 = weigh(1, j0, 256) + (j0,)
-            critic(j0, 256, (z01, z11), True)
+        for b in range(2):
+            for q in range(2):
+                first_products(b, q, 4 * b + 2 * q)
+        clip(0, 0, UNIT)
+        weigh(0, 0, UNIT, rounded[0])
+        clip(0, UNIT, UNIT)
+        weigh(0, UNIT, UNIT, rounded[0])
+        first_products(0, 2, 0)
+        clip(1, 0, HALF)
+        weigh(1, 0, HALF, rounded[1])
+        spent = ratio[0, 0][:].rearrange("p t j -> p (t j)").bitcast(BF16)
+        for b in range(2):
+            round_wc(b, 0, PACK, spent[:, b * PACK * HALF : (b + 1) * PACK * HALF], False)
+        first_products(1, 2, 2)
+        first_products(0, 3, 4)
+        first_products(1, 3, 6)
+        for n in range(4):
+            critic(banks[n], n, 1, 0, HALF, False)
+        clip(0, HALF, UNIT)
+        weigh(0, HALF, UNIT, rounded[0])
+        clip(1, HALF, UNIT)
+        weigh(1, HALF, UNIT, rounded[1])
+        for u in range(2):
+            critic(banks[4 + u], 2 * u, 2, HALF, UNIT, False)
+        clip(0, HALF + UNIT, UNIT)
+        weigh(0, HALF + UNIT, UNIT, rounded[0])
+        clip(1, HALF + UNIT, UNIT)
+        for g in range(2):
+            weigh(1, HALF + UNIT + g * P, P, rounded[1])
+            for u in range(2):
+                critic(banks[(6 + 2 * g + u) % 8], 2 * u, 2, HALF + UNIT + g * P, P, g == 1 and u == 1)

@@ -1,3 +1,4 @@
+import math
 from contextlib import ExitStack
 
 import concourse.mybir as mybir
@@ -22,6 +23,7 @@ PASS = P * PACK
 HALF = 512
 UNIT = 256
 CLIP = 2.0
+LOG_CLIP = math.log(CLIP)
 
 
 def tile_list_importance_weighted_critic_kernel(
@@ -48,13 +50,16 @@ def tile_list_importance_weighted_critic_kernel(
         rounded = [held("rounded%d" % i, [P, PACK * HALF], BF16) for i in range(4)]
         ratio = {(b, h): held("ratio%d%d" % (b, h), [P, PACK, HALF], F32) for b in range(2) for h in range(2)}
 
+        low = [buffer[:, : 2 * PASS] for buffer in rounded]
+        high = [buffer[:, 2 * PASS :] for buffer in rounded]
+
         def load_words(dst, src):
             nc.sync.dma_start(out=dst[:].bitcast(I32), in_=src.rearrange("p t i -> p (t i)").bitcast(I32))
 
-        def load_scales(dst, src, first):
+        def load_scales(dst, src, first, queue):
             passes = src.shape[0]
             for q in (0, 2, 1, 3):
-                nc.sync.dma_start(
+                queue.dma_start(
                     out=dst[32 * q + first : 32 * q + first + 4 * passes, :].bitcast(I32),
                     in_=src[:, 4 * q : 4 * q + 4, :].bitcast(I32),
                 )
@@ -76,6 +81,14 @@ def tile_list_importance_weighted_critic_kernel(
             for b in range(count):
                 wp_raw[a, b0 + b] = raw[:, :, blk(b)]
 
+        def load_wp_slots(raw, a, t0):
+            rows = wp[blk(a), :].rearrange("(p k) c -> p k c", k=PACK)
+            nc.sync.dma_start(out=raw[:, t0 : t0 + 2, :], in_=rows[:, t0 : t0 + 2, :])
+
+        def load_plane(dst, src):
+            for r in range(4):
+                nc.sync.dma_start(out=dst[r:P:32, :].bitcast(I32), in_=src[0, r:16:4, :].bitcast(I32))
+
         def load_adv(b, j0, width):
             raw = load_rows("adv%d_%d" % (b, j0), adv[blk(b), j0 : j0 + width])
             for j in range(j0, j0 + width, UNIT):
@@ -89,10 +102,14 @@ def tile_list_importance_weighted_critic_kernel(
         load_words(v2_words, tab2_words[0])
         nc.sync.dma_start(list1[:], offs)
         nc.sync.dma_start(out=wb_raw[:].bitcast(I32), in_=wb_words[0].bitcast(I32))
-        load_scales(v2_scales, tab2_scales, 0)
-        load_scales(v_scales, tab_scales, 4)
-        load_wp(0, 0, 2)
-        load_scales(wb_scales_raw, wb_scales, 0)
+        load_plane(v2_scales, tab2_scales)
+        wp_first = held("wp0", [P, PACK, H], F32)
+        for b in range(2):
+            wp_raw[0, b] = wp_first[:, :, blk(b)]
+        load_wp_slots(wp_first, 0, 0)
+        load_scales(v_scales, tab_scales, 4, nc.sync)
+        load_wp_slots(wp_first, 0, 2)
+        load_plane(wb_scales_raw, wb_scales)
         load_words(v_words[0], tab_words[0])
         load_wp(1, 0, 2)
         load_words(v_words[1], tab_words[1])
@@ -118,8 +135,8 @@ def tile_list_importance_weighted_critic_kernel(
             nc.vector.quantize_mx(out=codes[:].bitcast(FP8X4), scales=scales[:], in_=grouped)
             return [(codes[:, c : c + P], scales[:, c : c + P]) for c in range(0, width, P)]
 
-        def round_wp(a, b, t0, count, buffer, on_vector):
-            grouped = buffer[:, t0 * PASS : (t0 + count) * PASS]
+        def round_wp(a, b, t0, grouped, on_vector):
+            count = grouped.shape[1] // PASS
             dst = grouped.rearrange("p (t m k) -> p m k t", t=count, k=PACK)
             src = wp_raw[a, b].rearrange("p k (m t) -> p m k t", t=PACK)[:, :, :, t0 : t0 + count]
             if on_vector:
@@ -129,8 +146,8 @@ def tile_list_importance_weighted_critic_kernel(
             for t, operand in enumerate(quantize("wp%d%d%d" % (a, b, t0), grouped)):
                 wpq[a, b, t0 + t] = operand
 
-        def round_wc(b, n0, count, buffer, on_vector):
-            grouped = buffer[:, n0 * PASS : (n0 + count) * PASS]
+        def round_wc(b, n0, grouped, on_vector):
+            count = grouped.shape[1] // PASS
             dst = grouped.rearrange("p (c i k) -> p c k i", i=4, k=PACK)
             src = wc_raw[b][:, :, n0 * P : (n0 + count) * P].rearrange("p k (c i) -> p c k i", i=4)
             if on_vector:
@@ -162,17 +179,17 @@ def tile_list_importance_weighted_critic_kernel(
         g2s = gather("g2s", v2_scales, list2, 0, S, U8)
         g1s = gather("g1s", v_scales, list1, 0, S, U8)
         deal(wb_s[:], wb_scales_raw[:])
-        round_wp(0, 0, 0, PACK, rounded[0], False)
-        round_wp(0, 1, 0, PACK, rounded[1], False)
+        round_wp(0, 0, 0, rounded[0][:], False)
+        round_wp(0, 1, 0, rounded[1][:], False)
         gather_v(0, 0, S)
         for b in range(2):
-            round_wp(1, b, 0, 2, rounded[2 + b], False)
-            round_wp(1, b, 2, 2, rounded[2 + b], True)
+            round_wp(1, b, 0, low[2 + b], False)
+            round_wp(1, b, 2, high[2 + b], True)
         gather_v(1, 0, UNIT)
         gather_v(1, UNIT, UNIT)
         gather_v(1, HALF, HALF)
 
-        def first_products(b, q, first_bank):
+        def first_products(b, q, first_bank, clipped=False):
             cols = slice(q * UNIT, (q + 1) * UNIT)
             j0 = q % 2 * UNIT
             for u in range(2):
@@ -201,7 +218,12 @@ def tile_list_importance_weighted_critic_kernel(
                             stop=(a == 1 and e == 1),
                         )
                 target = ratio[b, q // 2][:, 2 * u : 2 * u + 2, j0 : j0 + UNIT]
-                nc.scalar.activation(target, bank[:].rearrange("p (e j) -> p e j", e=2), ACT.Exp, scale=-1.0)
+                source = bank[:].rearrange("p (e j) -> p e j", e=2)
+                if clipped:
+                    nc.scalar.activation(target, source, ACT.Relu, bias=LOG_CLIP)
+                    nc.scalar.activation(target, target, ACT.Exp, scale=-1.0, bias=LOG_CLIP)
+                else:
+                    nc.scalar.activation(target, source, ACT.Exp, scale=-1.0)
 
         z_codes = {}
         z_scales = {}
@@ -215,10 +237,9 @@ def tile_list_importance_weighted_critic_kernel(
             part = ratio[b, h][:, :, first : first + width]
             nc.vector.tensor_scalar(part, part, CLIP, None, ALU.min)
 
-        def weigh(b, j0, width, buffer):
+        def weigh(b, j0, width, grouped):
             h, first = divmod(j0, HALF)
             raw, start = adv_raw[b, j0 // UNIT]
-            grouped = buffer[:, PACK * first : PACK * (first + width)]
             nc.vector.tensor_tensor(
                 grouped.rearrange("p (c i t) -> p c t i", i=2, t=PACK),
                 ratio[b, h][:, :, first : first + width].rearrange("p t (c i) -> p c t i", i=2),
@@ -261,30 +282,31 @@ def tile_list_importance_weighted_critic_kernel(
             for q in range(2):
                 first_products(b, q, 4 * b + 2 * q)
         clip(0, 0, UNIT)
-        weigh(0, 0, UNIT, rounded[0])
+        weigh(0, 0, UNIT, low[0])
         clip(0, UNIT, UNIT)
-        weigh(0, UNIT, UNIT, rounded[0])
+        weigh(0, UNIT, UNIT, high[0])
         first_products(0, 2, 0)
         clip(1, 0, HALF)
-        weigh(1, 0, HALF, rounded[1])
+        weigh(1, 0, HALF, rounded[1][:])
         spent = ratio[0, 0][:].rearrange("p t j -> p (t j)").bitcast(BF16)
         for b in range(2):
-            round_wc(b, 0, PACK, spent[:, b * PACK * HALF : (b + 1) * PACK * HALF], False)
+            round_wc(b, 0, spent[:, b * PACK * HALF : (b + 1) * PACK * HALF], False)
         first_products(1, 2, 2)
         first_products(0, 3, 4)
-        first_products(1, 3, 6)
-        for n in range(4):
+        for n in range(2):
             critic(banks[n], n, 1, 0, HALF, False)
+        first_products(1, 3, 6, True)
+        for n in range(2, 4):
+            critic(banks[4 + n], n, 1, 0, HALF, False)
         clip(0, HALF, UNIT)
-        weigh(0, HALF, UNIT, rounded[0])
+        weigh(0, HALF, UNIT, low[0])
         clip(1, HALF, UNIT)
-        weigh(1, HALF, UNIT, rounded[1])
+        weigh(1, HALF, UNIT, low[1])
         for u in range(2):
             critic(banks[4 + u], 2 * u, 2, HALF, UNIT, False)
         clip(0, HALF + UNIT, UNIT)
-        weigh(0, HALF + UNIT, UNIT, rounded[0])
-        clip(1, HALF + UNIT, UNIT)
+        weigh(0, HALF + UNIT, UNIT, high[0])
         for g in range(2):
-            weigh(1, HALF + UNIT + g * P, P, rounded[1])
+            weigh(1, HALF + UNIT + g * P, P, high[1][:, g * PASS : (g + 1) * PASS])
             for u in range(2):
-                critic(banks[(6 + 2 * g + u) % 8], 2 * u, 2, HALF + UNIT + g * P, P, g == 1 and u == 1)
+                critic(banks[(6 + 2 * g + u) % 8], 2 * u, 2, HALF + UNIT + g * P, P, u == 1)

@@ -1,4 +1,3 @@
-import math
 from contextlib import ExitStack
 
 import concourse.mybir as mybir
@@ -23,7 +22,6 @@ PASS = P * PACK
 HALF = 512
 UNIT = 256
 CLIP = 2.0
-LOG_CLIP = math.log(CLIP)
 
 
 def tile_list_importance_weighted_critic_kernel(
@@ -189,7 +187,7 @@ def tile_list_importance_weighted_critic_kernel(
         gather_v(1, UNIT, UNIT)
         gather_v(1, HALF, HALF)
 
-        def first_products(b, q, first_bank, clipped=False):
+        def first_products(b, q, first_bank):
             cols = slice(q * UNIT, (q + 1) * UNIT)
             j0 = q % 2 * UNIT
             for u in range(2):
@@ -219,11 +217,7 @@ def tile_list_importance_weighted_critic_kernel(
                         )
                 target = ratio[b, q // 2][:, 2 * u : 2 * u + 2, j0 : j0 + UNIT]
                 source = bank[:].rearrange("p (e j) -> p e j", e=2)
-                if clipped:
-                    nc.scalar.activation(target, source, ACT.Relu, bias=LOG_CLIP)
-                    nc.scalar.activation(target, target, ACT.Exp, scale=-1.0, bias=LOG_CLIP)
-                else:
-                    nc.scalar.activation(target, source, ACT.Exp, scale=-1.0)
+                nc.scalar.activation(target, source, ACT.Exp, scale=-1.0)
 
         z_codes = {}
         z_scales = {}
@@ -295,7 +289,7 @@ def tile_list_importance_weighted_critic_kernel(
         first_products(0, 3, 4)
         for n in range(2):
             critic(banks[n], n, 1, 0, HALF, False)
-        first_products(1, 3, 6, True)
+        first_products(1, 3, 6)
         for n in range(2, 4):
             critic(banks[4 + n], n, 1, 0, HALF, False)
         clip(0, HALF, UNIT)
@@ -306,6 +300,7 @@ def tile_list_importance_weighted_critic_kernel(
             critic(banks[4 + u], 2 * u, 2, HALF, UNIT, False)
         clip(0, HALF + UNIT, UNIT)
         weigh(0, HALF + UNIT, UNIT, high[0])
+        clip(1, HALF + UNIT, UNIT)
         for g in range(2):
             weigh(1, HALF + UNIT + g * P, P, high[1][:, g * PASS : (g + 1) * PASS])
             for u in range(2):

@@ -92,15 +92,16 @@ def tile_list_importance_weighted_critic_kernel(
             for j in range(j0, j0 + width, UNIT):
                 adv_raw[b, j // UNIT] = (raw, j0)
 
-        nc.gpsimd.memset(v2_scales[:].bitcast(I32), 0)
+        nc.gpsimd.memset(v2_scales[:, : T // 2].bitcast(I32), 0)
+        nc.vector.memset(v2_scales[:, T // 2 :].bitcast(I32), 0)
         nc.vector.memset(v_scales[:].bitcast(I32), 0)
         nc.vector.memset(wb_scales_raw[:].bitcast(I32), 0)
 
         nc.sync.dma_start(list2[:], offs2)
-        load_words(v2_words, tab2_words[0])
         nc.sync.dma_start(list1[:], offs)
         nc.sync.dma_start(out=wb_raw[:].bitcast(I32), in_=wb_words[0].bitcast(I32))
         load_plane(v2_scales, tab2_scales)
+        load_words(v2_words, tab2_words[0])
         wp_first = held("wp0", [P, PACK, H], F32)
         for b in range(2):
             wp_raw[0, b] = wp_first[:, :, blk(b)]
@@ -172,17 +173,17 @@ def tile_list_importance_weighted_critic_kernel(
                 dst.rearrange("p (b t m) -> p b t m", b=2, t=PACK), src.rearrange("p (b m t) -> p b t m", b=2, t=PACK)
             )
 
-        g2w = gather("g2w", v2_words, list2, 0, S, U32)
         deal(wb_q[:].bitcast(U16), wb_raw[:].bitcast(U16))
         g2s = gather("g2s", v2_scales, list2, 0, S, U8)
+        g2w = gather("g2w", v2_words, list2, 0, S, U32)
         g1s = gather("g1s", v_scales, list1, 0, S, U8)
         deal(wb_s[:], wb_scales_raw[:])
         round_wp(0, 0, 0, rounded[0][:], False)
         round_wp(0, 1, 0, rounded[1][:], False)
         gather_v(0, 0, S)
-        for b in range(2):
-            round_wp(1, b, 0, low[2 + b], False)
-            round_wp(1, b, 2, high[2 + b], True)
+        round_wp(1, 0, 0, low[2], False)
+        round_wp(1, 0, 2, high[2], True)
+        round_wp(1, 1, 0, rounded[3][:], False)
         gather_v(1, 0, UNIT)
         gather_v(1, UNIT, UNIT)
         gather_v(1, HALF, HALF)
@@ -291,7 +292,7 @@ def tile_list_importance_weighted_critic_kernel(
             critic(banks[n], n, 1, 0, HALF, False)
         first_products(1, 3, 6)
         for n in range(2, 4):
-            critic(banks[4 + n], n, 1, 0, HALF, False)
+            critic(banks[n], n, 1, 0, HALF, False)
         clip(0, HALF, UNIT)
         weigh(0, HALF, UNIT, low[0])
         clip(1, HALF, UNIT)

@@ -263,13 +263,14 @@ def tile_list_importance_weighted_critic_kernel(
                     target = bank[:, e * width : (e + 1) * width]
                     critic_pass(target, b, n0 + e, j0, width, b == 0 and e == 0, b == 1 and e == count - 1)
             result = held("result%d_%d" % (j0, n0), [P, count, width], F32)
-            for e in range(count):
-                source = bank[:, e * width : (e + 1) * width]
-                column = bias[:, n0 + e : n0 + e + 1]
-                if on_vector:
-                    nc.vector.tensor_scalar(result[:, e, :], source, column, None, ALU.add)
-                else:
-                    nc.scalar.activation(result[:, e, :], source, ACT.Identity, bias=column)
+            if on_vector:
+                sums = bank[:, : count * width].rearrange("p (e j) -> p e j", e=count)
+                spread = bias[:, n0 : n0 + count].unsqueeze(2).to_broadcast([P, count, width])
+                nc.vector.tensor_tensor(result[:], sums, spread, ALU.add)
+            else:
+                for e in range(count):
+                    source = bank[:, e * width : (e + 1) * width]
+                    nc.scalar.activation(result[:, e, :], source, ACT.Identity, bias=bias[:, n0 + e : n0 + e + 1])
             rows = out[n0 * P : (n0 + count) * P, j0 : j0 + width]
             nc.sync.dma_start(out=rows.rearrange("(e p) j -> p e j", p=P), in_=result[:])
 
@@ -299,10 +300,10 @@ def tile_list_importance_weighted_critic_kernel(
         weigh(1, HALF, UNIT, low[1])
         for u in range(2):
             critic(banks[4 + u], 2 * u, 2, HALF, UNIT, False)
-        clip(0, HALF + UNIT, UNIT)
-        weigh(0, HALF + UNIT, UNIT, high[0])
-        clip(1, HALF + UNIT, UNIT)
+        for b in range(2):
+            clip(b, HALF + UNIT, UNIT)
         for g in range(2):
-            weigh(1, HALF + UNIT + g * P, P, high[1][:, g * PASS : (g + 1) * PASS])
+            for b in range(2):
+                weigh(b, HALF + UNIT + g * P, P, high[b][:, g * PASS : (g + 1) * PASS])
             for u in range(2):
                 critic(banks[(6 + 2 * g + u) % 8], 2 * u, 2, HALF + UNIT + g * P, P, u == 1)

@@ -83,32 +83,31 @@ def tile_list_importance_weighted_critic_kernel(
             rows = wp[blk(a), :].rearrange("(p k) c -> p k c", k=PACK)
             nc.sync.dma_start(out=raw[:, t0 : t0 + 2, :], in_=rows[:, t0 : t0 + 2, :])
 
-        def load_plane(dst, src):
+        def load_plane(dst, src, queue):
             for r in range(4):
-                nc.sync.dma_start(out=dst[r:P:32, :].bitcast(I32), in_=src[0, r:16:4, :].bitcast(I32))
+                queue.dma_start(out=dst[r:P:32, :].bitcast(I32), in_=src[0, r:16:4, :].bitcast(I32))
 
         def load_adv(b, j0, width):
             raw = load_rows("adv%d_%d" % (b, j0), adv[blk(b), j0 : j0 + width])
             for j in range(j0, j0 + width, UNIT):
                 adv_raw[b, j // UNIT] = (raw, j0)
 
-        nc.gpsimd.memset(v2_scales[:, : T // 2].bitcast(I32), 0)
-        nc.vector.memset(v2_scales[:, T // 2 :].bitcast(I32), 0)
+        nc.gpsimd.memset(v2_scales[:].bitcast(I32), 0)
         nc.vector.memset(v_scales[:].bitcast(I32), 0)
         nc.vector.memset(wb_scales_raw[:].bitcast(I32), 0)
 
         nc.sync.dma_start(list2[:], offs2)
+        load_words(v2_words, tab2_words[0])
         nc.sync.dma_start(list1[:], offs)
         nc.sync.dma_start(out=wb_raw[:].bitcast(I32), in_=wb_words[0].bitcast(I32))
-        load_plane(v2_scales, tab2_scales)
-        load_words(v2_words, tab2_words[0])
+        load_plane(v2_scales, tab2_scales, nc.scalar)
         wp_first = held("wp0", [P, PACK, H], F32)
         for b in range(2):
             wp_raw[0, b] = wp_first[:, :, blk(b)]
         load_wp_slots(wp_first, 0, 0)
         load_scales(v_scales, tab_scales, 4, nc.sync)
         load_wp_slots(wp_first, 0, 2)
-        load_plane(wb_scales_raw, wb_scales)
+        load_plane(wb_scales_raw, wb_scales, nc.sync)
         load_words(v_words[0], tab_words[0])
         load_wp(1, 0, 2)
         load_words(v_words[1], tab_words[1])
@@ -173,9 +172,9 @@ def tile_list_importance_weighted_critic_kernel(
                 dst.rearrange("p (b t m) -> p b t m", b=2, t=PACK), src.rearrange("p (b m t) -> p b t m", b=2, t=PACK)
             )
 
-        deal(wb_q[:].bitcast(U16), wb_raw[:].bitcast(U16))
         g2s = gather("g2s", v2_scales, list2, 0, S, U8)
         g2w = gather("g2w", v2_words, list2, 0, S, U32)
+        deal(wb_q[:].bitcast(U16), wb_raw[:].bitcast(U16))
         g1s = gather("g1s", v_scales, list1, 0, S, U8)
         deal(wb_s[:], wb_scales_raw[:])
         round_wp(0, 0, 0, rounded[0][:], False)

@@ -92,14 +92,14 @@ def tile_list_importance_weighted_critic_kernel(
             for j in range(j0, j0 + width, UNIT):
                 adv_raw[b, j // UNIT] = (raw, j0)
 
-        nc.gpsimd.memset(v2_scales[:].bitcast(I32), 0)
-        nc.vector.memset(v_scales[:].bitcast(I32), 0)
+        nc.gpsimd.memset(v_scales[:].bitcast(I32), 0)
+        nc.vector.memset(v2_scales[:].bitcast(I32), 0)
         nc.vector.memset(wb_scales_raw[:].bitcast(I32), 0)
 
         nc.sync.dma_start(list2[:], offs2)
+        nc.sync.dma_start(out=wb_raw[:].bitcast(I32), in_=wb_words[0].bitcast(I32))
         load_words(v2_words, tab2_words[0])
         nc.sync.dma_start(list1[:], offs)
-        nc.sync.dma_start(out=wb_raw[:].bitcast(I32), in_=wb_words[0].bitcast(I32))
         load_plane(v2_scales, tab2_scales, nc.scalar)
         wp_first = held("wp0", [P, PACK, H], F32)
         for b in range(2):
@@ -172,9 +172,9 @@ def tile_list_importance_weighted_critic_kernel(
                 dst.rearrange("p (b t m) -> p b t m", b=2, t=PACK), src.rearrange("p (b m t) -> p b t m", b=2, t=PACK)
             )
 
+        deal(wb_q[:].bitcast(U16), wb_raw[:].bitcast(U16))
         g2s = gather("g2s", v2_scales, list2, 0, S, U8)
         g2w = gather("g2w", v2_words, list2, 0, S, U32)
-        deal(wb_q[:].bitcast(U16), wb_raw[:].bitcast(U16))
         g1s = gather("g1s", v_scales, list1, 0, S, U8)
         deal(wb_s[:], wb_scales_raw[:])
         round_wp(0, 0, 0, rounded[0][:], False)

@@ -22,6 +22,7 @@ PASS = P * PACK
 HALF = 512
 UNIT = 256
 CLIP = 2.0
+WB = 2
 
 
 def tile_list_importance_weighted_critic_kernel(
@@ -32,8 +33,11 @@ def tile_list_importance_weighted_critic_kernel(
         keep = ctx.enter_context(tc.tile_pool(name="keep", bufs=1))
         psum = ctx.enter_context(tc.psum_pool(name="psum", bufs=1))
 
-        def held(name, shape, dtype):
-            return keep.tile(shape, dtype, name=name, align_bytes=64)
+        def held(name, shape, dtype, place=None):
+            return keep.tile(shape, dtype, name=name, tag=place or name, align_bytes=64)
+
+        def blk(i):
+            return slice(i * PASS, (i + 1) * PASS)
 
         list1 = held("list1", [P, S // 16], U16)
         list2 = held("list2", [P, S // 16], U16)
@@ -43,88 +47,73 @@ def tile_list_importance_weighted_critic_kernel(
         v2_scales = held("v2_scales", [P, T], U8)
         wb_raw = held("wb_raw", [P, 2 * H], U8)
         wb_scales_raw = held("wb_scales_raw", [P, H], U8)
+        wb_q = held("wb_q", [P, 2 * H], U8)
+        wb_s = held("wb_s", [P, H], U8)
         bias = held("bias", [P, N // P], F32)
         banks = [psum.tile([P, HALF], F32, name="bank%d" % i) for i in range(8)]
         rounded = [held("rounded%d" % i, [P, PACK * HALF], BF16) for i in range(4)]
-        ratio = {(b, h): held("ratio%d%d" % (b, h), [P, PACK, HALF], F32) for b in range(2) for h in range(2)}
-
-        low = [buffer[:, : 2 * PASS] for buffer in rounded]
-        high = [buffer[:, 2 * PASS :] for buffer in rounded]
+        ratio = [held("ratio%d" % b, [P, PACK * S], F32) for b in range(2)]
+        z_codes = [held("z_codes%d" % b, [P, S], U32) for b in range(2)]
+        z_scales = [held("z_scales%d" % b, [P, S], U8) for b in range(2)]
+        wp_raw = {}
+        adv_raw = {}
+        wc_raw = {}
+        wpq = {}
+        wcq = {}
+        g1w = {}
 
         def load_words(dst, src):
             nc.sync.dma_start(out=dst[:].bitcast(I32), in_=src.rearrange("p t i -> p (t i)").bitcast(I32))
 
-        def load_scales(dst, src, first, queue):
-            passes = src.shape[0]
-            for q in (0, 2, 1, 3):
+        def load_planes(dst, src, first, quadrants, queue):
+            for q in quadrants:
                 queue.dma_start(
-                    out=dst[32 * q + first : 32 * q + first + 4 * passes, :].bitcast(I32),
+                    out=dst[32 * q + first : 32 * q + first + 8, :].bitcast(I32),
                     in_=src[:, 4 * q : 4 * q + 4, :].bitcast(I32),
                 )
+
+        def load_plane(dst, src, queue):
+            for r in range(4):
+                queue.dma_start(out=dst[r:P:32, :].bitcast(I32), in_=src[0, r:16:4, :].bitcast(I32))
 
         def load_rows(name, src):
             raw = held(name, [P, PACK, src.shape[1]], F32)
             nc.sync.dma_start(out=raw[:], in_=src.rearrange("(p k) c -> p k c", k=PACK))
             return raw
 
-        def blk(i):
-            return slice(i * PASS, (i + 1) * PASS)
-
-        wp_raw = {}
-        adv_raw = {}
-        wc_raw = {}
-
         def load_wp(a, b0, count):
             raw = load_rows("wp%d%d" % (a, b0), wp[blk(a), b0 * PASS : (b0 + count) * PASS])
             for b in range(count):
                 wp_raw[a, b0 + b] = raw[:, :, blk(b)]
 
-        def load_wp_slots(raw, a, t0):
-            rows = wp[blk(a), :].rearrange("(p k) c -> p k c", k=PACK)
-            nc.sync.dma_start(out=raw[:, t0 : t0 + 2, :], in_=rows[:, t0 : t0 + 2, :])
-
-        def load_plane(dst, src, queue):
-            for r in range(4):
-                queue.dma_start(out=dst[r:P:32, :].bitcast(I32), in_=src[0, r:16:4, :].bitcast(I32))
-
         def load_adv(b, j0, width):
             raw = load_rows("adv%d_%d" % (b, j0), adv[blk(b), j0 : j0 + width])
-            for j in range(j0, j0 + width, UNIT):
-                adv_raw[b, j // UNIT] = (raw, j0)
+            for j in range(j0, j0 + width, P):
+                adv_raw[b, j // P] = (raw, j0)
 
-        nc.gpsimd.memset(v_scales[:].bitcast(I32), 0)
-        nc.vector.memset(v2_scales[:].bitcast(I32), 0)
-        nc.vector.memset(wb_scales_raw[:].bitcast(I32), 0)
+        def load_wc(b):
+            wc_raw[b] = load_rows("wc%d" % b, wc[blk(b), :])
 
-        nc.sync.dma_start(list2[:], offs2)
-        nc.sync.dma_start(out=wb_raw[:].bitcast(I32), in_=wb_words[0].bitcast(I32))
-        load_words(v2_words, tab2_words[0])
-        nc.sync.dma_start(list1[:], offs)
-        load_plane(v2_scales, tab2_scales, nc.scalar)
-        wp_first = held("wp0", [P, PACK, H], F32)
-        for b in range(2):
-            wp_raw[0, b] = wp_first[:, :, blk(b)]
-        load_wp_slots(wp_first, 0, 0)
-        load_scales(v_scales, tab_scales, 4, nc.sync)
-        load_wp_slots(wp_first, 0, 2)
-        load_plane(wb_scales_raw, wb_scales, nc.sync)
-        load_words(v_words[0], tab_words[0])
-        load_wp(1, 0, 2)
-        load_words(v_words[1], tab_words[1])
-        load_adv(0, 0, HALF)
-        load_adv(1, 0, HALF)
-        wc_raw[0] = load_rows("wc0", wc[blk(0), :])
-        wc_raw[1] = load_rows("wc1", wc[blk(1), :])
-        load_adv(0, HALF, HALF)
-        with nc.allow_non_contiguous_dma(reason="one bias value a partition"):
-            nc.sync.dma_start(out=bias[:], in_=bc.rearrange("(c p) -> p c", p=P))
-        load_adv(1, HALF, UNIT)
-        load_adv(1, HALF + UNIT, UNIT)
+        def load_bias():
+            with nc.allow_non_contiguous_dma(reason="one bias value a partition"):
+                nc.sync.dma_start(out=bias[:], in_=bc.rearrange("(c p) -> p c", p=P))
 
-        def gather(name, window, offsets, j0, width, dtype):
-            picked = held(name, [P, width], dtype)
+        def gather(name, window, offsets, j0, width, dtype, place=None):
+            picked = held(name, [P, width], dtype, place)
             nc.vector.tensor_copy(picked[:], window[:].indirect(offsets[:, j0 // 16 : (j0 + width) // 16]))
             return picked
+
+        def gather_v(a, j0, width, place=None):
+            picked = gather("g1w%d_%d" % (a, j0), v_words[a], list1, j0, width, U32, place)
+            for j in range(j0, j0 + width, P):
+                g1w[a, j // P] = picked[:, j - j0 : j - j0 + P]
+
+        def deal(dst, src):
+            blocks = src.shape[1] // PASS
+            nc.vector.tensor_copy(
+                dst.rearrange("p (b t m) -> p b t m", b=blocks, t=PACK),
+                src.rearrange("p (b m t) -> p b t m", b=blocks, t=PACK),
+            )
 
         def quantize(name, grouped):
             width = grouped.shape[1] // PACK
@@ -133,134 +122,88 @@ def tile_list_importance_weighted_critic_kernel(
             nc.vector.quantize_mx(out=codes[:].bitcast(FP8X4), scales=scales[:], in_=grouped)
             return [(codes[:, c : c + P], scales[:, c : c + P]) for c in range(0, width, P)]
 
-        def round_wp(a, b, t0, grouped, on_vector):
-            count = grouped.shape[1] // PASS
+        def round_wp(a, b, t0, count, buffer, on_vector):
+            grouped = buffer[:, t0 * PASS : (t0 + count) * PASS]
             dst = grouped.rearrange("p (t m k) -> p m k t", t=count, k=PACK)
             src = wp_raw[a, b].rearrange("p k (m t) -> p m k t", t=PACK)[:, :, :, t0 : t0 + count]
             if on_vector:
                 nc.vector.tensor_scalar(dst, src, -1.0, None, ALU.mult)
             else:
                 nc.scalar.activation(dst, src, ACT.Copy, scale=-1.0)
+
+        def quantize_wp(a, b, t0, count, buffer):
+            grouped = buffer[:, t0 * PASS : (t0 + count) * PASS]
             for t, operand in enumerate(quantize("wp%d%d%d" % (a, b, t0), grouped)):
                 wpq[a, b, t0 + t] = operand
 
-        def round_wc(b, n0, grouped, on_vector):
-            count = grouped.shape[1] // PASS
+        def round_wc(b, n0, count, buffer, on_vector):
+            grouped = buffer[:, n0 * PASS : (n0 + count) * PASS]
             dst = grouped.rearrange("p (c i k) -> p c k i", i=4, k=PACK)
             src = wc_raw[b][:, :, n0 * P : (n0 + count) * P].rearrange("p k (c i) -> p c k i", i=4)
             if on_vector:
                 nc.vector.tensor_copy(dst, src)
             else:
                 nc.scalar.activation(dst, src, ACT.Copy)
+
+        def quantize_wc(b, n0, count, buffer):
+            grouped = buffer[:, n0 * PASS : (n0 + count) * PASS]
             for n, operand in enumerate(quantize("wc%d%d" % (b, n0), grouped)):
                 wcq[b, n0 + n] = operand
 
-        wpq = {}
-        wcq = {}
-        g1w = {}
-
-        def gather_v(a, j0, width):
-            picked = gather("g1w%d_%d" % (a, j0), v_words[a], list1, j0, width, U32)
-            for j in range(j0, j0 + width, UNIT):
-                g1w[a, j // UNIT] = picked[:, j - j0 : j - j0 + UNIT]
-
-        wb_q = held("wb_q", [P, 2 * H], U8)
-        wb_s = held("wb_s", [P, H], U8)
-
-        def deal(dst, src):
-            nc.vector.tensor_copy(
-                dst.rearrange("p (b t m) -> p b t m", b=2, t=PACK), src.rearrange("p (b m t) -> p b t m", b=2, t=PACK)
-            )
-
-        deal(wb_q[:].bitcast(U16), wb_raw[:].bitcast(U16))
-        g2s = gather("g2s", v2_scales, list2, 0, S, U8)
-        g2w = gather("g2w", v2_words, list2, 0, S, U32)
-        g1s = gather("g1s", v_scales, list1, 0, S, U8)
-        deal(wb_s[:], wb_scales_raw[:])
-        round_wp(0, 0, 0, rounded[0][:], False)
-        round_wp(0, 1, 0, rounded[1][:], False)
-        gather_v(0, 0, S)
-        round_wp(1, 0, 0, low[2], False)
-        round_wp(1, 0, 2, high[2], True)
-        round_wp(1, 1, 0, rounded[3][:], False)
-        gather_v(1, 0, UNIT)
-        gather_v(1, UNIT, UNIT)
-        gather_v(1, HALF, HALF)
-
-        def first_products(b, q, first_bank):
-            cols = slice(q * UNIT, (q + 1) * UNIT)
-            j0 = q % 2 * UNIT
-            for u in range(2):
-                bank = banks[first_bank + u]
-                for e in range(2):
-                    c0 = b * PASS + (2 * u + e) * P
+        def first_products(b, g, bank, order):
+            cols = slice(g * P, (g + 1) * P)
+            for step, a in enumerate(order):
+                for t in range(PACK):
+                    if a == WB:
+                        c0 = b * PASS + t * P
+                        weights, weight_scales = wb_q[:, 2 * c0 : 2 * (c0 + P)].bitcast(FP4X4), wb_s[:, c0 : c0 + P]
+                        columns, column_scales = g2w[:, cols], g2s[:, cols]
+                    else:
+                        weights, weight_scales = wpq[a, b, t][0].bitcast(FP8X4), wpq[a, b, t][1]
+                        columns, column_scales = g1w[a, g], g1s[4 + 4 * a : P, cols]
                     nc.tensor.matmul_mx(
-                        out=bank[:, e * UNIT : (e + 1) * UNIT],
-                        lhsT=wb_q[:, 2 * c0 : 2 * (c0 + P)].bitcast(FP4X4),
-                        lhsT_scale=wb_s[:, c0 : c0 + P],
-                        rhs=g2w[:, cols].bitcast(FP8X4),
-                        rhs_scale=g2s[:, cols],
-                        start=(e == 0),
-                        stop=False,
+                        out=bank[:, t * P : (t + 1) * P],
+                        lhsT=weights,
+                        lhsT_scale=weight_scales,
+                        rhs=columns.bitcast(FP8X4),
+                        rhs_scale=column_scales,
+                        start=(step == 0 and t == 0),
+                        stop=(step == 2 and t == PACK - 1),
                     )
-                for a in range(2):
-                    for e in range(2):
-                        codes, scales = wpq[a, b, 2 * u + e]
-                        nc.tensor.matmul_mx(
-                            out=bank[:, e * UNIT : (e + 1) * UNIT],
-                            lhsT=codes.bitcast(FP8X4),
-                            lhsT_scale=scales,
-                            rhs=g1w[a, q].bitcast(FP8X4),
-                            rhs_scale=g1s[4 + 4 * a : P, cols],
-                            start=False,
-                            stop=(a == 1 and e == 1),
-                        )
-                target = ratio[b, q // 2][:, 2 * u : 2 * u + 2, j0 : j0 + UNIT]
-                source = bank[:].rearrange("p (e j) -> p e j", e=2)
-                nc.scalar.activation(target, source, ACT.Exp, scale=-1.0)
-
-        z_codes = {}
-        z_scales = {}
-        for b in range(2):
-            for h in range(2):
-                z_codes[b, h] = held("z_codes%d%d" % (b, h), [P, HALF], U32)
-                z_scales[b, h] = held("z_scales%d%d" % (b, h), [P, HALF], U8)
-
-        def clip(b, j0, width):
-            h, first = divmod(j0, HALF)
-            part = ratio[b, h][:, :, first : first + width]
-            nc.vector.tensor_scalar(part, part, CLIP, None, ALU.min)
+            target = ratio[b][:, g * PASS : (g + 1) * PASS].rearrange("p (j t) -> p j t", t=PACK)
+            nc.scalar.activation(target, bank[:].rearrange("p (t j) -> p j t", t=PACK), ACT.Exp, scale=-1.0)
 
         def weigh(b, j0, width, grouped):
-            h, first = divmod(j0, HALF)
-            raw, start = adv_raw[b, j0 // UNIT]
-            nc.vector.tensor_tensor(
-                grouped.rearrange("p (c i t) -> p c t i", i=2, t=PACK),
-                ratio[b, h][:, :, first : first + width].rearrange("p t (c i) -> p c t i", i=2),
-                raw[:, :, j0 - start : j0 - start + width].rearrange("p t (c i) -> p c t i", i=2),
+            raw, start = adv_raw[b, j0 // P]
+            nc.vector.scalar_tensor_tensor(
+                grouped[:, : PACK * width].rearrange("p (j t) -> p j t", t=PACK),
+                ratio[b][:, PACK * j0 : PACK * (j0 + width)].rearrange("p (j t) -> p j t", t=PACK),
+                CLIP,
+                raw[:, :, j0 - start : j0 - start + width].rearrange("p t j -> p j t"),
+                ALU.min,
                 ALU.mult,
             )
-            cols = slice(first, first + width)
-            nc.vector.quantize_mx(out=z_codes[b, h][:, cols].bitcast(FP8X4), scales=z_scales[b, h][:, cols], in_=grouped)
 
-        def critic_pass(target, b, n, j0, width, start, stop):
-            codes, scales = wcq[b, n]
-            cols = slice(j0 % HALF, j0 % HALF + width)
-            nc.tensor.matmul_mx(
-                out=target,
-                lhsT=codes.bitcast(FP8X4),
-                lhsT_scale=scales,
-                rhs=z_codes[b, j0 // HALF][:, cols].bitcast(FP8X4),
-                rhs_scale=z_scales[b, j0 // HALF][:, cols],
-                start=start,
-                stop=stop,
+        def quantize_z(b, j0, width, grouped):
+            cols = slice(j0, j0 + width)
+            nc.vector.quantize_mx(
+                out=z_codes[b][:, cols].bitcast(FP8X4), scales=z_scales[b][:, cols], in_=grouped[:, : PACK * width]
             )
 
         def critic(bank, n0, count, j0, width, on_vector):
+            cols = slice(j0, j0 + width)
             for b in range(2):
                 for e in range(count):
-                    target = bank[:, e * width : (e + 1) * width]
-                    critic_pass(target, b, n0 + e, j0, width, b == 0 and e == 0, b == 1 and e == count - 1)
+                    codes, scales = wcq[b, n0 + e]
+                    nc.tensor.matmul_mx(
+                        out=bank[:, e * width : (e + 1) * width],
+                        lhsT=codes.bitcast(FP8X4),
+                        lhsT_scale=scales,
+                        rhs=z_codes[b][:, cols].bitcast(FP8X4),
+                        rhs_scale=z_scales[b][:, cols],
+                        start=(b == 0 and e == 0),
+                        stop=(b == 1 and e == count - 1),
+                    )
             result = held("result%d_%d" % (j0, n0), [P, count, width], F32)
             if on_vector:
                 sums = bank[:, : count * width].rearrange("p (e j) -> p e j", e=count)
@@ -273,36 +216,81 @@ def tile_list_importance_weighted_critic_kernel(
             rows = out[n0 * P : (n0 + count) * P, j0 : j0 + width]
             nc.sync.dma_start(out=rows.rearrange("(e p) j -> p e j", p=P), in_=result[:])
 
-        for b in range(2):
-            for q in range(2):
-                first_products(b, q, 4 * b + 2 * q)
-        clip(0, 0, UNIT)
-        weigh(0, 0, UNIT, low[0])
-        clip(0, UNIT, UNIT)
-        weigh(0, UNIT, UNIT, high[0])
-        first_products(0, 2, 0)
-        clip(1, 0, HALF)
-        weigh(1, 0, HALF, rounded[1][:])
-        spent = ratio[0, 0][:].rearrange("p t j -> p (t j)").bitcast(BF16)
-        for b in range(2):
-            round_wc(b, 0, spent[:, b * PACK * HALF : (b + 1) * PACK * HALF], False)
-        first_products(1, 2, 2)
-        first_products(0, 3, 4)
-        for n in range(2):
+        nc.vector.memset(v2_scales[:].bitcast(I32), 0)
+        nc.vector.memset(wb_scales_raw[:].bitcast(I32), 0)
+        nc.gpsimd.memset(v_scales[:].bitcast(I32), 0)
+
+        nc.sync.dma_start(list2[:], offs2)
+        nc.sync.dma_start(out=wb_raw[:].bitcast(I32), in_=wb_words[0].bitcast(I32))
+        load_words(v2_words, tab2_words[0])
+        nc.sync.dma_start(list1[:], offs)
+        load_wp(0, 0, 1)
+        load_bias()
+        load_plane(v2_scales, tab2_scales, nc.scalar)
+        load_words(v_words[0], tab_words[0])
+        load_plane(wb_scales_raw, wb_scales, nc.sync)
+        load_planes(v_scales, tab_scales, 4, (0, 2), nc.sync)
+        load_wp(1, 0, 1)
+        load_planes(v_scales, tab_scales, 4, (1, 3), nc.sync)
+        load_wp(0, 1, 1)
+        load_words(v_words[1], tab_words[1])
+        load_wp(1, 1, 1)
+        load_adv(0, 0, HALF)
+        load_adv(1, 0, HALF)
+        load_wc(0)
+        load_wc(1)
+        load_adv(0, HALF, HALF)
+        load_adv(1, HALF, UNIT)
+        load_adv(1, HALF + UNIT, UNIT)
+
+        deal(wb_q[:].bitcast(U16), wb_raw[:].bitcast(U16))
+        g2s = gather("g2s", v2_scales, list2, 0, S, U8)
+        g2w = gather("g2w", v2_words, list2, 0, S, U32)
+        deal(wb_s[:], wb_scales_raw[:])
+        gather_v(0, 0, S)
+        round_wp(0, 0, 0, 4, rounded[0], False)
+        quantize_wp(0, 0, 0, 4, rounded[0])
+        g1s = gather("g1s", v_scales, list1, 0, S, U8)
+        round_wp(1, 0, 0, 4, rounded[1], False)
+        quantize_wp(1, 0, 0, 4, rounded[1])
+        round_wp(0, 1, 0, 4, rounded[2], False)
+        gather_v(1, 0, UNIT)
+        gather_v(1, UNIT, UNIT)
+        quantize_wp(0, 1, 0, 4, rounded[2])
+        gather_v(1, HALF, HALF)
+        for g in range(4):
+            first_products(0, g, banks[g], (WB, 0, 1))
+        round_wp(1, 1, 0, 4, rounded[0], True)
+        quantize_wp(1, 1, 0, 4, rounded[0])
+        for g in range(4):
+            first_products(1, g, banks[4 + g], (WB, 0, 1))
+        for g in range(4, 8):
+            first_products(0, g, banks[g - 4], (WB, 0, 1))
+        weigh(0, 0, HALF, rounded[1])
+        weigh(1, 0, HALF, rounded[2])
+        quantize_z(0, 0, HALF, rounded[1])
+        quantize_z(1, 0, HALF, rounded[2])
+        spent = ratio[1][:, : PACK * UNIT].bitcast(BF16)
+        round_wc(0, 0, 4, spent, False)
+        for g in range(4, 8):
+            first_products(1, g, banks[g], (WB, 0, 1))
+        round_wc(1, 0, 4, rounded[3], True)
+        quantize_wc(1, 0, 4, rounded[3])
+        quantize_wc(0, 0, 4, spent)
+        for n in range(4):
             critic(banks[n], n, 1, 0, HALF, False)
-        first_products(1, 3, 6)
-        for n in range(2, 4):
-            critic(banks[n], n, 1, 0, HALF, False)
-        clip(0, HALF, UNIT)
-        weigh(0, HALF, UNIT, low[0])
-        clip(1, HALF, UNIT)
-        weigh(1, HALF, UNIT, low[1])
+        weigh(0, HALF, UNIT, rounded[2])
+        weigh(1, HALF, UNIT, rounded[1])
+        quantize_z(0, HALF, UNIT, rounded[2])
+        weigh(0, HALF + UNIT, UNIT, rounded[0])
+        quantize_z(1, HALF, UNIT, rounded[1])
         for u in range(2):
             critic(banks[4 + u], 2 * u, 2, HALF, UNIT, False)
-        for b in range(2):
-            clip(b, HALF + UNIT, UNIT)
+        weigh(1, HALF + UNIT, P, rounded[3])
+        quantize_z(0, HALF + UNIT, UNIT, rounded[0])
+        weigh(1, HALF + UNIT + P, P, rounded[2])
+        quantize_z(1, HALF + UNIT, P, rounded[3])
+        quantize_z(1, HALF + UNIT + P, P, rounded[2])
         for g in range(2):
-            for b in range(2):
-                weigh(b, HALF + UNIT + g * P, P, high[b][:, g * PASS : (g + 1) * PASS])
             for u in range(2):
                 critic(banks[(6 + 2 * g + u) % 8], 2 * u, 2, HALF + UNIT + g * P, P, u == 1)

@@ -51,8 +51,9 @@ def tile_list_importance_weighted_critic_kernel(
         wb_s = held("wb_s", [P, H], U8)
         bias = held("bias", [P, N // P], F32)
         banks = [psum.tile([P, HALF], F32, name="bank%d" % i) for i in range(8)]
-        rounded = [held("rounded%d" % i, [P, PACK * HALF], BF16) for i in range(4)]
-        ratio = [held("ratio%d" % b, [P, PACK * S], F32) for b in range(2)]
+        rounded = [held("rounded%d" % i, [P, PACK * HALF], BF16) for i in range(3)]
+        pairs = [held("pairs%d" % i, [P, PACK * HALF], BF16) for i in range(2)]
+        ratio = {(b, u): held("ratio%d%d" % (b, u), [P, 2 * S], F32) for b in range(2) for u in range(2)}
         z_codes = [held("z_codes%d" % b, [P, S], U32) for b in range(2)]
         z_scales = [held("z_scales%d" % b, [P, S], U8) for b in range(2)]
         wp_raw = {}
@@ -105,8 +106,8 @@ def tile_list_importance_weighted_critic_kernel(
 
         def gather_v(a, j0, width, place=None):
             picked = gather("g1w%d_%d" % (a, j0), v_words[a], list1, j0, width, U32, place)
-            for j in range(j0, j0 + width, P):
-                g1w[a, j // P] = picked[:, j - j0 : j - j0 + P]
+            for j in range(j0, j0 + width, UNIT):
+                g1w[a, j // UNIT] = picked[:, j - j0 : j - j0 + UNIT]
 
         def deal(dst, src):
             blocks = src.shape[1] // PASS
@@ -150,39 +151,49 @@ def tile_list_importance_weighted_critic_kernel(
             for n, operand in enumerate(quantize("wc%d%d" % (b, n0), grouped)):
                 wcq[b, n0 + n] = operand
 
-        def first_products(b, g, bank, order):
-            cols = slice(g * P, (g + 1) * P)
-            for step, a in enumerate(order):
-                for t in range(PACK):
-                    if a == WB:
-                        c0 = b * PASS + t * P
-                        weights, weight_scales = wb_q[:, 2 * c0 : 2 * (c0 + P)].bitcast(FP4X4), wb_s[:, c0 : c0 + P]
-                        columns, column_scales = g2w[:, cols], g2s[:, cols]
-                    else:
-                        weights, weight_scales = wpq[a, b, t][0].bitcast(FP8X4), wpq[a, b, t][1]
-                        columns, column_scales = g1w[a, g], g1s[4 + 4 * a : P, cols]
-                    nc.tensor.matmul_mx(
-                        out=bank[:, t * P : (t + 1) * P],
-                        lhsT=weights,
-                        lhsT_scale=weight_scales,
-                        rhs=columns.bitcast(FP8X4),
-                        rhs_scale=column_scales,
-                        start=(step == 0 and t == 0),
-                        stop=(step == 2 and t == PACK - 1),
-                    )
-            target = ratio[b][:, g * PASS : (g + 1) * PASS].rearrange("p (j t) -> p j t", t=PACK)
-            nc.scalar.activation(target, bank[:].rearrange("p (t j) -> p j t", t=PACK), ACT.Exp, scale=-1.0)
+        def first_products(b, q, first_bank, order):
+            cols = slice(q * UNIT, (q + 1) * UNIT)
+            for u in range(2):
+                bank = banks[first_bank + u]
+                for step, a in enumerate(order):
+                    for e in range(2):
+                        t = 2 * u + e
+                        if a == WB:
+                            c0 = b * PASS + t * P
+                            weights, weight_scales = wb_q[:, 2 * c0 : 2 * (c0 + P)].bitcast(FP4X4), wb_s[:, c0 : c0 + P]
+                            columns, column_scales = g2w[:, cols], g2s[:, cols]
+                        else:
+                            weights, weight_scales = wpq[a, b, t][0].bitcast(FP8X4), wpq[a, b, t][1]
+                            columns, column_scales = g1w[a, q], g1s[4 + 4 * a : P, cols]
+                        nc.tensor.matmul_mx(
+                            out=bank[:, e * UNIT : (e + 1) * UNIT],
+                            lhsT=weights,
+                            lhsT_scale=weight_scales,
+                            rhs=columns.bitcast(FP8X4),
+                            rhs_scale=column_scales,
+                            start=(step == 0 and e == 0),
+                            stop=(step == 2 and e == 1),
+                        )
+                target = ratio[b, u][:, 2 * q * UNIT : 2 * (q + 1) * UNIT].rearrange("p (j e) -> p j e", e=2)
+                nc.scalar.activation(target, bank[:].rearrange("p (e j) -> p j e", e=2), ACT.Exp, scale=-1.0)
 
-        def weigh(b, j0, width, grouped):
+        def weigh(b, j0, width, buffer, span=None):
             raw, start = adv_raw[b, j0 // P]
-            nc.vector.scalar_tensor_tensor(
-                grouped[:, : PACK * width].rearrange("p (j t) -> p j t", t=PACK),
-                ratio[b][:, PACK * j0 : PACK * (j0 + width)].rearrange("p (j t) -> p j t", t=PACK),
-                CLIP,
-                raw[:, :, j0 - start : j0 - start + width].rearrange("p t j -> p j t"),
-                ALU.min,
-                ALU.mult,
-            )
+            span = span or width
+            for u in range(2):
+                first = 2 * (u * span + j0 % span)
+                nc.vector.scalar_tensor_tensor(
+                    buffer[:, first : first + 2 * width].rearrange("p (j e) -> p j e", e=2),
+                    ratio[b, u][:, 2 * j0 : 2 * (j0 + width)].rearrange("p (j e) -> p j e", e=2),
+                    CLIP,
+                    raw[:, 2 * u : 2 * u + 2, j0 - start : j0 - start + width].rearrange("p e j -> p j e"),
+                    ALU.min,
+                    ALU.mult,
+                )
+
+        def weave(width, buffer, grouped):
+            words = buffer[:, : PACK * width].bitcast(I32).rearrange("p (u j) -> p j u", u=2)
+            nc.vector.tensor_copy(grouped[:, : PACK * width].bitcast(I32).rearrange("p (j u) -> p j u", u=2), words)
 
         def quantize_z(b, j0, width, grouped):
             cols = slice(j0, j0 + width)
@@ -216,17 +227,17 @@ def tile_list_importance_weighted_critic_kernel(
             rows = out[n0 * P : (n0 + count) * P, j0 : j0 + width]
             nc.sync.dma_start(out=rows.rearrange("(e p) j -> p e j", p=P), in_=result[:])
 
-        nc.vector.memset(v2_scales[:].bitcast(I32), 0)
+        nc.gpsimd.memset(v2_scales[:].bitcast(I32), 0)
         nc.vector.memset(wb_scales_raw[:].bitcast(I32), 0)
-        nc.gpsimd.memset(v_scales[:].bitcast(I32), 0)
+        nc.vector.memset(v_scales[:].bitcast(I32), 0)
 
         nc.sync.dma_start(list2[:], offs2)
         nc.sync.dma_start(out=wb_raw[:].bitcast(I32), in_=wb_words[0].bitcast(I32))
         load_words(v2_words, tab2_words[0])
         nc.sync.dma_start(list1[:], offs)
-        load_wp(0, 0, 1)
         load_bias()
-        load_plane(v2_scales, tab2_scales, nc.scalar)
+        load_plane(v2_scales, tab2_scales, nc.sync)
+        load_wp(0, 0, 1)
         load_words(v_words[0], tab_words[0])
         load_plane(wb_scales_raw, wb_scales, nc.sync)
         load_planes(v_scales, tab_scales, 4, (0, 2), nc.sync)
@@ -238,8 +249,9 @@ def tile_list_importance_weighted_critic_kernel(
         load_adv(0, 0, HALF)
         load_adv(1, 0, HALF)
         load_wc(0)
+        load_adv(0, HALF, UNIT)
         load_wc(1)
-        load_adv(0, HALF, HALF)
+        load_adv(0, HALF + UNIT, UNIT)
         load_adv(1, HALF, UNIT)
         load_adv(1, HALF + UNIT, UNIT)
 
@@ -250,46 +262,56 @@ def tile_list_importance_weighted_critic_kernel(
         gather_v(0, 0, S)
         round_wp(0, 0, 0, 4, rounded[0], False)
         quantize_wp(0, 0, 0, 4, rounded[0])
-        g1s = gather("g1s", v_scales, list1, 0, S, U8)
+        g1s = gather("g1s", v_scales, list1, 0, S, U8, "wb_scales_raw")
         round_wp(1, 0, 0, 4, rounded[1], False)
         quantize_wp(1, 0, 0, 4, rounded[1])
-        round_wp(0, 1, 0, 4, rounded[2], False)
+        early = held("early", [P, PACK * HALF], BF16)
+        round_wp(0, 1, 0, 4, early, False)
         gather_v(1, 0, UNIT)
         gather_v(1, UNIT, UNIT)
-        quantize_wp(0, 1, 0, 4, rounded[2])
-        gather_v(1, HALF, HALF)
-        for g in range(4):
-            first_products(0, g, banks[g], (WB, 0, 1))
+        quantize_wp(0, 1, 0, 4, early)
+        gather_v(1, HALF, HALF, "early")
+        for q in range(2):
+            first_products(0, q, 2 * q, (WB, 0, 1))
         round_wp(1, 1, 0, 4, rounded[0], True)
         quantize_wp(1, 1, 0, 4, rounded[0])
-        for g in range(4):
-            first_products(1, g, banks[4 + g], (WB, 0, 1))
-        for g in range(4, 8):
-            first_products(0, g, banks[g - 4], (WB, 0, 1))
-        weigh(0, 0, HALF, rounded[1])
-        weigh(1, 0, HALF, rounded[2])
+        for q in range(2):
+            first_products(1, q, 4 + 2 * q, (WB, 0, 1))
+        for q in range(2, 4):
+            first_products(0, q, 2 * (q - 2), (WB, 0, 1))
+        weigh(0, 0, HALF, pairs[0])
+        weave(HALF, pairs[0], rounded[1])
+        weigh(1, 0, HALF, pairs[1])
         quantize_z(0, 0, HALF, rounded[1])
+        weave(HALF, pairs[1], rounded[2])
+        spent = [ratio[1, u][:, : PACK * UNIT].bitcast(BF16) for u in range(2)]
+        round_wc(0, 0, 4, spent[0], False)
+        first_products(1, 2, 4, (WB, 0, 1))
+        weigh(0, HALF, UNIT, pairs[0])
         quantize_z(1, 0, HALF, rounded[2])
-        spent = ratio[1][:, : PACK * UNIT].bitcast(BF16)
-        round_wc(0, 0, 4, spent, False)
-        for g in range(4, 8):
-            first_products(1, g, banks[g], (WB, 0, 1))
-        round_wc(1, 0, 4, rounded[3], True)
-        quantize_wc(1, 0, 4, rounded[3])
-        quantize_wc(0, 0, 4, spent)
+        quantize_wc(0, 0, 4, spent[0])
+        weave(UNIT, pairs[0], rounded[1])
+        round_wc(1, 0, 2, spent[1], False)
+        round_wc(1, 2, 2, spent[1], False)
+        first_products(1, 3, 6, (WB, 0, 1))
+        weigh(0, HALF + UNIT, UNIT, pairs[1])
+        quantize_z(0, HALF, UNIT, rounded[1])
+        quantize_wc(1, 0, 2, spent[1])
+        weave(UNIT, pairs[1], rounded[2])
+        quantize_wc(1, 2, 2, spent[1])
         for n in range(4):
             critic(banks[n], n, 1, 0, HALF, False)
-        weigh(0, HALF, UNIT, rounded[2])
-        weigh(1, HALF, UNIT, rounded[1])
-        quantize_z(0, HALF, UNIT, rounded[2])
-        weigh(0, HALF + UNIT, UNIT, rounded[0])
-        quantize_z(1, HALF, UNIT, rounded[1])
+        weigh(1, HALF, UNIT, pairs[0])
+        quantize_z(0, HALF + UNIT, UNIT, rounded[2])
+        weave(UNIT, pairs[0], rounded[0])
+        weigh(1, HALF + UNIT, P, pairs[1])
+        quantize_z(1, HALF, UNIT, rounded[0])
+        weave(P, pairs[1], rounded[1])
         for u in range(2):
             critic(banks[4 + u], 2 * u, 2, HALF, UNIT, False)
-        weigh(1, HALF + UNIT, P, rounded[3])
-        quantize_z(0, HALF + UNIT, UNIT, rounded[0])
-        weigh(1, HALF + UNIT + P, P, rounded[2])
-        quantize_z(1, HALF + UNIT, P, rounded[3])
+        weigh(1, HALF + UNIT + P, P, pairs[0])
+        quantize_z(1, HALF + UNIT, P, rounded[1])
+        weave(P, pairs[0], rounded[2])
         quantize_z(1, HALF + UNIT + P, P, rounded[2])
         for g in range(2):
             for u in range(2):

@@ -104,10 +104,15 @@ def tile_list_importance_weighted_critic_kernel(
             nc.vector.tensor_copy(picked[:], window[:].indirect(offsets[:, j0 // 16 : (j0 + width) // 16]))
             return picked
 
-        def gather_v(a, j0, width, place=None):
-            picked = gather("g1w%d_%d" % (a, j0), v_words[a], list1, j0, width, U32, place)
-            for j in range(j0, j0 + width, UNIT):
-                g1w[a, j // UNIT] = picked[:, j - j0 : j - j0 + UNIT]
+        def gather_v(a, j0, widths, place=None):
+            picked = held("g1w%d_%d" % (a, j0), [P, sum(widths)], U32, place)
+            first = 0
+            for width in widths:
+                offsets = list1[:, (j0 + first) // 16 : (j0 + first + width) // 16]
+                nc.vector.tensor_copy(picked[:, first : first + width], v_words[a][:].indirect(offsets))
+                first = first + width
+            for j in range(0, first, UNIT):
+                g1w[a, (j0 + j) // UNIT] = picked[:, j : j + UNIT]
 
         def deal(dst, src):
             blocks = src.shape[1] // PASS
@@ -137,8 +142,7 @@ def tile_list_importance_weighted_critic_kernel(
             for t, operand in enumerate(quantize("wp%d%d%d" % (a, b, t0), grouped)):
                 wpq[a, b, t0 + t] = operand
 
-        def round_wc(b, n0, count, buffer, on_vector):
-            grouped = buffer[:, n0 * PASS : (n0 + count) * PASS]
+        def round_wc(b, n0, count, grouped, on_vector):
             dst = grouped.rearrange("p (c i k) -> p c k i", i=4, k=PACK)
             src = wc_raw[b][:, :, n0 * P : (n0 + count) * P].rearrange("p k (c i) -> p c k i", i=4)
             if on_vector:
@@ -146,8 +150,7 @@ def tile_list_importance_weighted_critic_kernel(
             else:
                 nc.scalar.activation(dst, src, ACT.Copy)
 
-        def quantize_wc(b, n0, count, buffer):
-            grouped = buffer[:, n0 * PASS : (n0 + count) * PASS]
+        def quantize_wc(b, n0, count, grouped):
             for n, operand in enumerate(quantize("wc%d%d" % (b, n0), grouped)):
                 wcq[b, n0 + n] = operand
 
@@ -191,9 +194,14 @@ def tile_list_importance_weighted_critic_kernel(
                     ALU.mult,
                 )
 
-        def weave(width, buffer, grouped):
-            words = buffer[:, : PACK * width].bitcast(I32).rearrange("p (u j) -> p j u", u=2)
-            nc.vector.tensor_copy(grouped[:, : PACK * width].bitcast(I32).rearrange("p (j u) -> p j u", u=2), words)
+        def weave(width, buffer, grouped, on_vector=True):
+            word = I32 if on_vector else U32
+            words = buffer[:, : PACK * width].bitcast(word).rearrange("p (u j) -> p j u", u=2)
+            woven = grouped[:, : PACK * width].bitcast(word).rearrange("p (j u) -> p j u", u=2)
+            if on_vector:
+                nc.vector.tensor_copy(woven, words)
+            else:
+                nc.scalar.copy(woven, words)
 
         def quantize_z(b, j0, width, grouped):
             cols = slice(j0, j0 + width)
@@ -201,7 +209,7 @@ def tile_list_importance_weighted_critic_kernel(
                 out=z_codes[b][:, cols].bitcast(FP8X4), scales=z_scales[b][:, cols], in_=grouped[:, : PACK * width]
             )
 
-        def critic(bank, n0, count, j0, width, on_vector):
+        def critic(bank, result, n0, count, j0, width, on_vector):
             cols = slice(j0, j0 + width)
             for b in range(2):
                 for e in range(count):
@@ -215,17 +223,22 @@ def tile_list_importance_weighted_critic_kernel(
                         start=(b == 0 and e == 0),
                         stop=(b == 1 and e == count - 1),
                     )
-            result = held("result%d_%d" % (j0, n0), [P, count, width], F32)
             if on_vector:
                 sums = bank[:, : count * width].rearrange("p (e j) -> p e j", e=count)
                 spread = bias[:, n0 : n0 + count].unsqueeze(2).to_broadcast([P, count, width])
-                nc.vector.tensor_tensor(result[:], sums, spread, ALU.add)
+                nc.vector.tensor_tensor(result, sums, spread, ALU.add)
             else:
                 for e in range(count):
                     source = bank[:, e * width : (e + 1) * width]
                     nc.scalar.activation(result[:, e, :], source, ACT.Identity, bias=bias[:, n0 + e : n0 + e + 1])
-            rows = out[n0 * P : (n0 + count) * P, j0 : j0 + width]
-            nc.sync.dma_start(out=rows.rearrange("(e p) j -> p e j", p=P), in_=result[:])
+
+        def finish(first_bank, n0, tiles, count, j0, width, vector_from, queue=nc.sync):
+            result = held("result%d_%d" % (j0, n0), [P, tiles, width], F32)
+            for i, n in enumerate(range(0, tiles, count)):
+                bank = banks[(first_bank + i) % 8]
+                critic(bank, result[:, n : n + count, :], n0 + n, count, j0, width, i >= vector_from)
+            rows = out[n0 * P : (n0 + tiles) * P, j0 : j0 + width]
+            queue.dma_start(out=rows.rearrange("(e p) j -> p e j", p=P), in_=result[:])
 
         nc.gpsimd.memset(v2_scales[:].bitcast(I32), 0)
         nc.vector.memset(wb_scales_raw[:].bitcast(I32), 0)
@@ -251,15 +264,15 @@ def tile_list_importance_weighted_critic_kernel(
         load_wc(0)
         load_adv(0, HALF, UNIT)
         load_wc(1)
-        load_adv(0, HALF + UNIT, UNIT)
         load_adv(1, HALF, UNIT)
+        load_adv(0, HALF + UNIT, UNIT)
         load_adv(1, HALF + UNIT, UNIT)
 
         deal(wb_q[:].bitcast(U16), wb_raw[:].bitcast(U16))
         g2s = gather("g2s", v2_scales, list2, 0, S, U8)
         g2w = gather("g2w", v2_words, list2, 0, S, U32)
         deal(wb_s[:], wb_scales_raw[:])
-        gather_v(0, 0, S)
+        gather_v(0, 0, [S])
         round_wp(0, 0, 0, 4, rounded[0], False)
         quantize_wp(0, 0, 0, 4, rounded[0])
         g1s = gather("g1s", v_scales, list1, 0, S, U8, "wb_scales_raw")
@@ -267,10 +280,10 @@ def tile_list_importance_weighted_critic_kernel(
         quantize_wp(1, 0, 0, 4, rounded[1])
         early = held("early", [P, PACK * HALF], BF16)
         round_wp(0, 1, 0, 4, early, False)
-        gather_v(1, 0, UNIT)
-        gather_v(1, UNIT, UNIT)
+        gather_v(1, 0, [UNIT])
+        gather_v(1, UNIT, [UNIT])
         quantize_wp(0, 1, 0, 4, early)
-        gather_v(1, HALF, HALF, "early")
+        gather_v(1, HALF, [HALF], "early")
         for q in range(2):
             first_products(0, q, 2 * q, (WB, 0, 1))
         round_wp(1, 1, 0, 4, rounded[0], True)
@@ -281,38 +294,39 @@ def tile_list_importance_weighted_critic_kernel(
             first_products(0, q, 2 * (q - 2), (WB, 0, 1))
         weigh(0, 0, HALF, pairs[0])
         weave(HALF, pairs[0], rounded[1])
-        weigh(1, 0, HALF, pairs[1])
+        weigh(1, 0, UNIT, pairs[1], HALF)
         quantize_z(0, 0, HALF, rounded[1])
+        weigh(1, UNIT, UNIT, pairs[1], HALF)
         weave(HALF, pairs[1], rounded[2])
-        spent = [ratio[1, u][:, : PACK * UNIT].bitcast(BF16) for u in range(2)]
-        round_wc(0, 0, 4, spent[0], False)
-        first_products(1, 2, 4, (WB, 0, 1))
-        weigh(0, HALF, UNIT, pairs[0])
-        quantize_z(1, 0, HALF, rounded[2])
-        quantize_wc(0, 0, 4, spent[0])
-        weave(UNIT, pairs[0], rounded[1])
-        round_wc(1, 0, 2, spent[1], False)
-        round_wc(1, 2, 2, spent[1], False)
-        first_products(1, 3, 6, (WB, 0, 1))
-        weigh(0, HALF + UNIT, UNIT, pairs[1])
-        quantize_z(0, HALF, UNIT, rounded[1])
-        quantize_wc(1, 0, 2, spent[1])
-        weave(UNIT, pairs[1], rounded[2])
-        quantize_wc(1, 2, 2, spent[1])
-        for n in range(4):
-            critic(banks[n], n, 1, 0, HALF, False)
-        weigh(1, HALF, UNIT, pairs[0])
-        quantize_z(0, HALF + UNIT, UNIT, rounded[2])
-        weave(UNIT, pairs[0], rounded[0])
-        weigh(1, HALF + UNIT, P, pairs[1])
-        quantize_z(1, HALF, UNIT, rounded[0])
-        weave(P, pairs[1], rounded[1])
-        for u in range(2):
-            critic(banks[4 + u], 2 * u, 2, HALF, UNIT, False)
-        weigh(1, HALF + UNIT + P, P, pairs[0])
-        quantize_z(1, HALF + UNIT, P, rounded[1])
-        weave(P, pairs[0], rounded[2])
-        quantize_z(1, HALF + UNIT + P, P, rounded[2])
-        for g in range(2):
+        spent = {}
+        for b in range(2):
             for u in range(2):
-                critic(banks[(6 + 2 * g + u) % 8], 2 * u, 2, HALF + UNIT + g * P, P, u == 1)
+                spent[b, u] = ratio[1, u][:, b * PASS : (b + 1) * PASS].bitcast(BF16)
+                round_wc(b, 2 * u, 2, spent[b, u], False)
+            first_products(1, 2 + b, 4 + 2 * b, (WB, 0, 1))
+        quantize_z(1, 0, HALF, rounded[2])
+        for u in range(2):
+            quantize_wc(0, 2 * u, 2, spent[0, u])
+        weigh(0, HALF, UNIT, pairs[0])
+        weave(UNIT, pairs[0], rounded[0])
+        weigh(1, HALF, UNIT, pairs[1])
+        quantize_wc(1, 0, 2, spent[1, 0])
+        quantize_z(0, HALF, UNIT, rounded[0])
+        weave(UNIT, pairs[1], rounded[1])
+        quantize_wc(1, 2, 2, spent[1, 1])
+        for n in range(4):
+            finish(0 + n, n, 1, 1, 0, HALF, 1)
+        weigh(0, HALF + UNIT, UNIT, pairs[0])
+        quantize_z(1, HALF, UNIT, rounded[1])
+        for u in range(2):
+            finish(4 + u, 2 * u, 2, 2, HALF, UNIT, 1)
+        weave(UNIT, pairs[0], rounded[2])
+        weigh(1, HALF + UNIT, P, pairs[1])
+        quantize_z(0, HALF + UNIT, UNIT, rounded[2])
+        weave(P, pairs[1], rounded[0])
+        weigh(1, HALF + UNIT + P, P, pairs[0])
+        quantize_z(1, HALF + UNIT, P, rounded[0])
+        weave(P, pairs[0], rounded[1])
+        quantize_z(1, HALF + UNIT + P, P, rounded[1])
+        for g in range(2):
+            finish(6 + 2 * g, 0, 4, 2, HALF + UNIT + g * P, P, 1)

@@ -52,10 +52,10 @@ def tile_list_importance_weighted_critic_kernel(
         bias = held("bias", [P, N // P], F32)
         banks = [psum.tile([P, HALF], F32, name="bank%d" % i) for i in range(8)]
         rounded = [held("rounded%d" % i, [P, PACK * HALF], BF16) for i in range(3)]
-        pairs = [held("pairs%d" % i, [P, PACK * HALF], BF16) for i in range(2)]
+        pairs = held("pairs", [P, 2 * PACK * HALF], BF16)
+        woven = held("woven", [P, 2 * PACK * HALF], BF16)
         ratio = {(b, u): held("ratio%d%d" % (b, u), [P, 2 * S], F32) for b in range(2) for u in range(2)}
-        z_codes = [held("z_codes%d" % b, [P, S], U32) for b in range(2)]
-        z_scales = [held("z_scales%d" % b, [P, S], U8) for b in range(2)]
+        zq = {}
         wp_raw = {}
         adv_raw = {}
         wc_raw = {}
@@ -114,6 +114,10 @@ def tile_list_importance_weighted_critic_kernel(
             for j in range(0, first, UNIT):
                 g1w[a, (j0 + j) // UNIT] = picked[:, j : j + UNIT]
 
+        def gather_scales(j0, width):
+            offsets = list1[:, j0 // 16 : (j0 + width) // 16]
+            nc.vector.tensor_copy(g1s[:, j0 : j0 + width], v_scales[:].indirect(offsets))
+
         def deal(dst, src):
             blocks = src.shape[1] // PASS
             nc.vector.tensor_copy(
@@ -154,37 +158,59 @@ def tile_list_importance_weighted_critic_kernel(
             for n, operand in enumerate(quantize("wc%d%d" % (b, n0), grouped)):
                 wcq[b, n0 + n] = operand
 
-        def first_products(b, q, first_bank, order):
-            cols = slice(q * UNIT, (q + 1) * UNIT)
-            for u in range(2):
-                bank = banks[first_bank + u]
-                for step, a in enumerate(order):
-                    for e in range(2):
-                        t = 2 * u + e
-                        if a == WB:
-                            c0 = b * PASS + t * P
-                            weights, weight_scales = wb_q[:, 2 * c0 : 2 * (c0 + P)].bitcast(FP4X4), wb_s[:, c0 : c0 + P]
-                            columns, column_scales = g2w[:, cols], g2s[:, cols]
-                        else:
-                            weights, weight_scales = wpq[a, b, t][0].bitcast(FP8X4), wpq[a, b, t][1]
-                            columns, column_scales = g1w[a, q], g1s[4 + 4 * a : P, cols]
-                        nc.tensor.matmul_mx(
-                            out=bank[:, e * UNIT : (e + 1) * UNIT],
-                            lhsT=weights,
-                            lhsT_scale=weight_scales,
-                            rhs=columns.bitcast(FP8X4),
-                            rhs_scale=column_scales,
-                            start=(step == 0 and e == 0),
-                            stop=(step == 2 and e == 1),
-                        )
-                target = ratio[b, u][:, 2 * q * UNIT : 2 * (q + 1) * UNIT].rearrange("p (j e) -> p j e", e=2)
-                nc.scalar.activation(target, bank[:].rearrange("p (e j) -> p j e", e=2), ACT.Exp, scale=-1.0)
+        def products(b, t0, slots, j0, width, bank, passes=(WB, 0, 1)):
+            cols = slice(j0, j0 + width)
+            inner = slice(j0 % UNIT, j0 % UNIT + width)
+            for a in passes:
+                for e in range(slots):
+                    t = t0 + e
+                    if a == WB:
+                        c0 = b * PASS + t * P
+                        weights, weight_scales = wb_q[:, 2 * c0 : 2 * (c0 + P)].bitcast(FP4X4), wb_s[:, c0 : c0 + P]
+                        columns, column_scales = g2w[:, cols], g2s[:, cols]
+                    else:
+                        weights, weight_scales = wpq[a, b, t][0].bitcast(FP8X4), wpq[a, b, t][1]
+                        columns, column_scales = g1w[a, j0 // UNIT][:, inner], g1s[4 + 4 * a : P, cols]
+                    nc.tensor.matmul_mx(
+                        out=bank[:, e * width : (e + 1) * width],
+                        lhsT=weights,
+                        lhsT_scale=weight_scales,
+                        rhs=columns.bitcast(FP8X4),
+                        rhs_scale=column_scales,
+                        start=(a == WB and e == 0),
+                        stop=(a == 1 and e == slots - 1),
+                    )
 
-        def weigh(b, j0, width, buffer, span=None):
+        def exponential(target, bank, slots):
+            woven_ratios = target.rearrange("p (j e) -> p j e", e=slots)
+            nc.scalar.activation(woven_ratios, bank[:].rearrange("p (e j) -> p j e", e=slots), ACT.Exp, scale=-1.0)
+
+        def first_products(b, q, first_bank, halves=(0, 1), passes=(WB, 0, 1)):
+            for u in halves:
+                products(b, 2 * u, 2, q * UNIT, UNIT, banks[first_bank + u], passes)
+                exponential(ratio[b, u][:, q * PASS : (q + 1) * PASS], banks[first_bank + u], 2)
+
+        def last_products(b, q, first_bank):
+            for g in range(2):
+                products(b, 0, PACK, q * UNIT + g * P, P, banks[first_bank + g])
+                exponential(ratio[b, g][:, q * PASS : (q + 1) * PASS], banks[first_bank + g], PACK)
+
+        def weigh_whole(b, q, g, grouped):
+            j0 = q * UNIT + g * P
             raw, start = adv_raw[b, j0 // P]
-            span = span or width
+            nc.vector.scalar_tensor_tensor(
+                grouped.rearrange("p (j t) -> p j t", t=PACK),
+                ratio[b, g][:, q * PASS : (q + 1) * PASS].rearrange("p (j t) -> p j t", t=PACK),
+                CLIP,
+                raw[:, :, j0 - start : j0 - start + P].rearrange("p t j -> p j t"),
+                ALU.min,
+                ALU.mult,
+            )
+
+        def weigh(b, j0, width, buffer, place, span=None):
+            raw, start = adv_raw[b, j0 // P]
             for u in range(2):
-                first = 2 * (u * span + j0 % span)
+                first = 2 * ((2 * place + u) * (span or width) + j0 % (span or width))
                 nc.vector.scalar_tensor_tensor(
                     buffer[:, first : first + 2 * width].rearrange("p (j e) -> p j e", e=2),
                     ratio[b, u][:, 2 * j0 : 2 * (j0 + width)].rearrange("p (j e) -> p j e", e=2),
@@ -194,23 +220,21 @@ def tile_list_importance_weighted_critic_kernel(
                     ALU.mult,
                 )
 
-        def weave(width, buffer, grouped, on_vector=True):
-            word = I32 if on_vector else U32
-            words = buffer[:, : PACK * width].bitcast(word).rearrange("p (u j) -> p j u", u=2)
-            woven = grouped[:, : PACK * width].bitcast(word).rearrange("p (j u) -> p j u", u=2)
-            if on_vector:
-                nc.vector.tensor_copy(woven, words)
-            else:
-                nc.scalar.copy(woven, words)
+        def weave(buffer, grouped, blocks):
+            words = buffer.bitcast(I32).rearrange("p (b u j) -> p b j u", b=blocks, u=2)
+            nc.vector.tensor_copy(grouped.bitcast(I32).rearrange("p (b j u) -> p b j u", b=blocks, u=2), words)
 
-        def quantize_z(b, j0, width, grouped):
-            cols = slice(j0, j0 + width)
-            nc.vector.quantize_mx(
-                out=z_codes[b][:, cols].bitcast(FP8X4), scales=z_scales[b][:, cols], in_=grouped[:, : PACK * width]
-            )
+        def quantize_z(blocks, j0, grouped, pieces=1):
+            count = len(blocks) * pieces
+            width = grouped.shape[1] // (count * PACK)
+            codes = held("z_codes%d_%d" % (blocks[0], j0), [P, count * width], U32)
+            scales = held("z_scales%d_%d" % (blocks[0], j0), [P, count * width], U8)
+            nc.vector.quantize_mx(out=codes[:].bitcast(FP8X4), scales=scales[:], in_=grouped)
+            for i in range(count):
+                cols = slice(i * width, (i + 1) * width)
+                zq[blocks[i // pieces], j0 + i % pieces * width] = (codes[:, cols], scales[:, cols])
 
         def critic(bank, result, n0, count, j0, width, on_vector):
-            cols = slice(j0, j0 + width)
             for b in range(2):
                 for e in range(count):
                     codes, scales = wcq[b, n0 + e]
@@ -218,8 +242,8 @@ def tile_list_importance_weighted_critic_kernel(
                         out=bank[:, e * width : (e + 1) * width],
                         lhsT=codes.bitcast(FP8X4),
                         lhsT_scale=scales,
-                        rhs=z_codes[b][:, cols].bitcast(FP8X4),
-                        rhs_scale=z_scales[b][:, cols],
+                        rhs=zq[b, j0][0].bitcast(FP8X4),
+                        rhs_scale=zq[b, j0][1],
                         start=(b == 0 and e == 0),
                         stop=(b == 1 and e == count - 1),
                     )
@@ -241,26 +265,26 @@ def tile_list_importance_weighted_critic_kernel(
             queue.dma_start(out=rows.rearrange("(e p) j -> p e j", p=P), in_=result[:])
 
         nc.gpsimd.memset(v2_scales[:].bitcast(I32), 0)
-        nc.vector.memset(wb_scales_raw[:].bitcast(I32), 0)
         nc.vector.memset(v_scales[:].bitcast(I32), 0)
+        nc.vector.memset(wb_scales_raw[:].bitcast(I32), 0)
 
         nc.sync.dma_start(list2[:], offs2)
-        nc.sync.dma_start(out=wb_raw[:].bitcast(I32), in_=wb_words[0].bitcast(I32))
-        load_words(v2_words, tab2_words[0])
         nc.sync.dma_start(list1[:], offs)
-        load_bias()
+        nc.sync.dma_start(out=wb_raw[:].bitcast(I32), in_=wb_words[0].bitcast(I32))
         load_plane(v2_scales, tab2_scales, nc.sync)
-        load_wp(0, 0, 1)
+        load_words(v2_words, tab2_words[0])
         load_words(v_words[0], tab_words[0])
-        load_plane(wb_scales_raw, wb_scales, nc.sync)
+        load_planes(v_scales, tab_scales, 4, (1, 3), nc.gpsimd)
+        load_wp(0, 0, 1)
         load_planes(v_scales, tab_scales, 4, (0, 2), nc.sync)
+        load_plane(wb_scales_raw, wb_scales, nc.sync)
         load_wp(1, 0, 1)
-        load_planes(v_scales, tab_scales, 4, (1, 3), nc.sync)
         load_wp(0, 1, 1)
         load_words(v_words[1], tab_words[1])
         load_wp(1, 1, 1)
         load_adv(0, 0, HALF)
         load_adv(1, 0, HALF)
+        load_bias()
         load_wc(0)
         load_adv(0, HALF, UNIT)
         load_wc(1)
@@ -270,7 +294,7 @@ def tile_list_importance_weighted_critic_kernel(
 
         deal(wb_q[:].bitcast(U16), wb_raw[:].bitcast(U16))
         g2s = gather("g2s", v2_scales, list2, 0, S, U8)
-        g2w = gather("g2w", v2_words, list2, 0, S, U32)
+        g2w = gather("g2w", v2_words, list2, 0, S, U32, "v2_scales")
         deal(wb_s[:], wb_scales_raw[:])
         gather_v(0, 0, [S])
         round_wp(0, 0, 0, 4, rounded[0], False)
@@ -285,48 +309,50 @@ def tile_list_importance_weighted_critic_kernel(
         quantize_wp(0, 1, 0, 4, early)
         gather_v(1, HALF, [HALF], "early")
         for q in range(2):
-            first_products(0, q, 2 * q, (WB, 0, 1))
+            first_products(0, q, 2 * q)
         round_wp(1, 1, 0, 4, rounded[0], True)
         quantize_wp(1, 1, 0, 4, rounded[0])
         for q in range(2):
-            first_products(1, q, 4 + 2 * q, (WB, 0, 1))
+            first_products(1, q, 4 + 2 * q)
         for q in range(2, 4):
-            first_products(0, q, 2 * (q - 2), (WB, 0, 1))
-        weigh(0, 0, HALF, pairs[0])
-        weave(HALF, pairs[0], rounded[1])
-        weigh(1, 0, UNIT, pairs[1], HALF)
-        quantize_z(0, 0, HALF, rounded[1])
-        weigh(1, UNIT, UNIT, pairs[1], HALF)
-        weave(HALF, pairs[1], rounded[2])
+            first_products(0, q, 2 * (q - 2))
+        half = [slice(b * PACK * HALF, (b + 1) * PACK * HALF) for b in range(2)]
+        weigh(0, 0, HALF, pairs, 0)
+        weave(pairs[:, half[0]], woven[:, half[0]], 1)
+        weigh(1, 0, UNIT, pairs, 1, HALF)
+        quantize_z((0,), 0, woven[:, half[0]])
+        weigh(1, UNIT, UNIT, pairs, 1, HALF)
+        weave(pairs[:, half[1]], woven[:, half[1]], 1)
         spent = {}
         for b in range(2):
             for u in range(2):
                 spent[b, u] = ratio[1, u][:, b * PASS : (b + 1) * PASS].bitcast(BF16)
                 round_wc(b, 2 * u, 2, spent[b, u], False)
-            first_products(1, 2 + b, 4 + 2 * b, (WB, 0, 1))
-        quantize_z(1, 0, HALF, rounded[2])
+            (first_products, last_products)[b](1, 2 + b, 4 + 2 * b)
+        quantize_z((1,), 0, woven[:, half[1]])
         for u in range(2):
             quantize_wc(0, 2 * u, 2, spent[0, u])
-        weigh(0, HALF, UNIT, pairs[0])
-        weave(UNIT, pairs[0], rounded[0])
-        weigh(1, HALF, UNIT, pairs[1])
+        low = [buffer[:, : 2 * PASS] for buffer in rounded]
+        high = [buffer[:, 2 * PASS :] for buffer in rounded]
+        eighth = [rounded[2][:, (2 + g) * PASS : (3 + g) * PASS] for g in range(2)]
+        weigh(0, HALF, UNIT, rounded[0], 0)
+        weave(low[0], low[1], 1)
+        weigh(1, HALF, UNIT, rounded[0], 1)
         quantize_wc(1, 0, 2, spent[1, 0])
-        quantize_z(0, HALF, UNIT, rounded[0])
-        weave(UNIT, pairs[1], rounded[1])
+        quantize_z((0,), HALF, low[1])
+        weave(high[0], high[1], 1)
         quantize_wc(1, 2, 2, spent[1, 1])
         for n in range(4):
-            finish(0 + n, n, 1, 1, 0, HALF, 1)
-        weigh(0, HALF + UNIT, UNIT, pairs[0])
-        quantize_z(1, HALF, UNIT, rounded[1])
+            finish(n, n, 1, 1, 0, HALF, 1)
+        weigh(0, HALF + UNIT, UNIT, low[2], 0)
+        quantize_z((1,), HALF, high[1])
         for u in range(2):
             finish(4 + u, 2 * u, 2, 2, HALF, UNIT, 1)
-        weave(UNIT, pairs[0], rounded[2])
-        weigh(1, HALF + UNIT, P, pairs[1])
-        quantize_z(0, HALF + UNIT, UNIT, rounded[2])
-        weave(P, pairs[1], rounded[0])
-        weigh(1, HALF + UNIT + P, P, pairs[0])
-        quantize_z(1, HALF + UNIT, P, rounded[0])
-        weave(P, pairs[0], rounded[1])
-        quantize_z(1, HALF + UNIT + P, P, rounded[1])
+        weave(low[2], low[0], 1)
+        weigh_whole(1, 3, 0, eighth[0])
+        quantize_z((0,), HALF + UNIT, low[0], 2)
+        weigh_whole(1, 3, 1, eighth[1])
+        for g in range(2):
+            quantize_z((1,), HALF + UNIT + g * P, eighth[g])
         for g in range(2):
             finish(6 + 2 * g, 0, 4, 2, HALF + UNIT + g * P, P, 1)

@@ -319,16 +319,15 @@ def tile_list_importance_weighted_critic_kernel(
         half = [slice(b * PACK * HALF, (b + 1) * PACK * HALF) for b in range(2)]
         weigh(0, 0, HALF, pairs, 0)
         weave(pairs[:, half[0]], woven[:, half[0]], 1)
-        weigh(1, 0, UNIT, pairs, 1, HALF)
+        weigh(1, 0, HALF, pairs, 1)
         quantize_z((0,), 0, woven[:, half[0]])
-        weigh(1, UNIT, UNIT, pairs, 1, HALF)
         weave(pairs[:, half[1]], woven[:, half[1]], 1)
         spent = {}
         for b in range(2):
             for u in range(2):
-                spent[b, u] = ratio[1, u][:, b * PASS : (b + 1) * PASS].bitcast(BF16)
+                spent[b, u] = ratio[b, u][:, :PASS].bitcast(BF16)
                 round_wc(b, 2 * u, 2, spent[b, u], False)
-            (first_products, last_products)[b](1, 2 + b, 4 + 2 * b)
+            first_products(1, 2 + b, 4 + 2 * b)
         quantize_z((1,), 0, woven[:, half[1]])
         for u in range(2):
             quantize_wc(0, 2 * u, 2, spent[0, u])
@@ -349,10 +348,12 @@ def tile_list_importance_weighted_critic_kernel(
         for u in range(2):
             finish(4 + u, 2 * u, 2, 2, HALF, UNIT, 1)
         weave(low[2], low[0], 1)
-        weigh_whole(1, 3, 0, eighth[0])
+        weigh(1, HALF + UNIT, P, eighth[0], 0)
         quantize_z((0,), HALF + UNIT, low[0], 2)
-        weigh_whole(1, 3, 1, eighth[1])
-        for g in range(2):
-            quantize_z((1,), HALF + UNIT + g * P, eighth[g])
+        weave(eighth[0], pairs[:, :PASS], 1)
+        weigh(1, HALF + UNIT + P, P, eighth[1], 0)
+        quantize_z((1,), HALF + UNIT, pairs[:, :PASS])
+        weave(eighth[1], woven[:, :PASS], 1)
+        quantize_z((1,), HALF + UNIT + P, woven[:, :PASS])
         for g in range(2):
             finish(6 + 2 * g, 0, 4, 2, HALF + UNIT + g * P, P, 1)

@@ -54,7 +54,19 @@ def tile_list_importance_weighted_critic_kernel(
         rounded = [held("rounded%d" % i, [P, PACK * HALF], BF16) for i in range(3)]
         pairs = held("pairs", [P, 2 * PACK * HALF], BF16)
         woven = held("woven", [P, 2 * PACK * HALF], BF16)
-        ratio = {(b, u): held("ratio%d%d" % (b, u), [P, 2 * S], F32) for b in range(2) for u in range(2)}
+        ratio = {}
+
+        def hold_ratios(b, h, place=None):
+            both = held("ratio%d%d" % (b, h), [P, 2 * S], F32, place)
+            for u in range(2):
+                ratio[b, h, u] = both[:, u * S : (u + 1) * S]
+
+        def ratios(b, u, j0, width):
+            first = 2 * (j0 % HALF)
+            return ratio[b, j0 // HALF, u][:, first : first + 2 * width]
+
+        for b, h in ((0, 0), (0, 1), (1, 0)):
+            hold_ratios(b, h)
         zq = {}
         wp_raw = {}
         adv_raw = {}
@@ -188,32 +200,15 @@ def tile_list_importance_weighted_critic_kernel(
         def first_products(b, q, first_bank, halves=(0, 1), passes=(WB, 0, 1)):
             for u in halves:
                 products(b, 2 * u, 2, q * UNIT, UNIT, banks[first_bank + u], passes)
-                exponential(ratio[b, u][:, q * PASS : (q + 1) * PASS], banks[first_bank + u], 2)
+                exponential(ratios(b, u, q * UNIT, UNIT), banks[first_bank + u], 2)
 
-        def last_products(b, q, first_bank):
-            for g in range(2):
-                products(b, 0, PACK, q * UNIT + g * P, P, banks[first_bank + g])
-                exponential(ratio[b, g][:, q * PASS : (q + 1) * PASS], banks[first_bank + g], PACK)
-
-        def weigh_whole(b, q, g, grouped):
-            j0 = q * UNIT + g * P
+        def weigh(b, j0, width, buffer, place, span=None, slot_pairs=(0, 1)):
             raw, start = adv_raw[b, j0 // P]
-            nc.vector.scalar_tensor_tensor(
-                grouped.rearrange("p (j t) -> p j t", t=PACK),
-                ratio[b, g][:, q * PASS : (q + 1) * PASS].rearrange("p (j t) -> p j t", t=PACK),
-                CLIP,
-                raw[:, :, j0 - start : j0 - start + P].rearrange("p t j -> p j t"),
-                ALU.min,
-                ALU.mult,
-            )
-
-        def weigh(b, j0, width, buffer, place, span=None):
-            raw, start = adv_raw[b, j0 // P]
-            for u in range(2):
+            for u in slot_pairs:
                 first = 2 * ((2 * place + u) * (span or width) + j0 % (span or width))
                 nc.vector.scalar_tensor_tensor(
                     buffer[:, first : first + 2 * width].rearrange("p (j e) -> p j e", e=2),
-                    ratio[b, u][:, 2 * j0 : 2 * (j0 + width)].rearrange("p (j e) -> p j e", e=2),
+                    ratios(b, u, j0, width).rearrange("p (j e) -> p j e", e=2),
                     CLIP,
                     raw[:, 2 * u : 2 * u + 2, j0 - start : j0 - start + width].rearrange("p e j -> p j e"),
                     ALU.min,
@@ -286,8 +281,8 @@ def tile_list_importance_weighted_critic_kernel(
         load_adv(1, 0, HALF)
         load_bias()
         load_wc(0)
-        load_adv(0, HALF, UNIT)
         load_wc(1)
+        load_adv(0, HALF, UNIT)
         load_adv(1, HALF, UNIT)
         load_adv(0, HALF + UNIT, UNIT)
         load_adv(1, HALF + UNIT, UNIT)
@@ -325,24 +320,26 @@ def tile_list_importance_weighted_critic_kernel(
         spent = {}
         for b in range(2):
             for u in range(2):
-                spent[b, u] = ratio[b, u][:, :PASS].bitcast(BF16)
+                spent[b, u] = ratios(b, u, 0, UNIT).bitcast(BF16)
                 round_wc(b, 2 * u, 2, spent[b, u], False)
-            first_products(1, 2 + b, 4 + 2 * b)
+        hold_ratios(1, 1, "wc1")
+        first_products(1, 2, 4)
         quantize_z((1,), 0, woven[:, half[1]])
         for u in range(2):
             quantize_wc(0, 2 * u, 2, spent[0, u])
         low = [buffer[:, : 2 * PASS] for buffer in rounded]
         high = [buffer[:, 2 * PASS :] for buffer in rounded]
         eighth = [rounded[2][:, (2 + g) * PASS : (3 + g) * PASS] for g in range(2)]
+        for u in range(2):
+            quantize_wc(1, 2 * u, 2, spent[1, u])
+        for n in range(4):
+            finish(n, n, 1, 1, 0, HALF, 1)
+        first_products(1, 3, 6)
         weigh(0, HALF, UNIT, rounded[0], 0)
         weave(low[0], low[1], 1)
         weigh(1, HALF, UNIT, rounded[0], 1)
-        quantize_wc(1, 0, 2, spent[1, 0])
         quantize_z((0,), HALF, low[1])
         weave(high[0], high[1], 1)
-        quantize_wc(1, 2, 2, spent[1, 1])
-        for n in range(4):
-            finish(n, n, 1, 1, 0, HALF, 1)
         weigh(0, HALF + UNIT, UNIT, low[2], 0)
         quantize_z((1,), HALF, high[1])
         for u in range(2):

@@ -126,13 +126,9 @@ def tile_list_importance_weighted_critic_kernel(
             for j in range(0, first, UNIT):
                 g1w[a, (j0 + j) // UNIT] = picked[:, j : j + UNIT]
 
-        def gather_scales(j0, width):
-            offsets = list1[:, j0 // 16 : (j0 + width) // 16]
-            nc.vector.tensor_copy(g1s[:, j0 : j0 + width], v_scales[:].indirect(offsets))
-
-        def deal(dst, src):
+        def deal(dst, src, move):
             blocks = src.shape[1] // PASS
-            nc.vector.tensor_copy(
+            move(
                 dst.rearrange("p (b t m) -> p b t m", b=blocks, t=PACK),
                 src.rearrange("p (b m t) -> p b t m", b=blocks, t=PACK),
             )
@@ -287,14 +283,15 @@ def tile_list_importance_weighted_critic_kernel(
         load_adv(0, HALF + UNIT, UNIT)
         load_adv(1, HALF + UNIT, UNIT)
 
-        deal(wb_q[:].bitcast(U16), wb_raw[:].bitcast(U16))
+        deal(wb_q[:].bitcast(U16), wb_raw[:].bitcast(U16), nc.scalar.copy)
         g2s = gather("g2s", v2_scales, list2, 0, S, U8)
         g2w = gather("g2w", v2_words, list2, 0, S, U32, "v2_scales")
-        deal(wb_s[:], wb_scales_raw[:])
+        for b in range(2):
+            deal(wb_s[:, blk(b)], wb_scales_raw[:, blk(b)], nc.gpsimd.tensor_copy)
         gather_v(0, 0, [S])
         round_wp(0, 0, 0, 4, rounded[0], False)
         quantize_wp(0, 0, 0, 4, rounded[0])
-        g1s = gather("g1s", v_scales, list1, 0, S, U8, "wb_scales_raw")
+        g1s = gather("g1s", v_scales, list1, 0, S, U8)
         round_wp(1, 0, 0, 4, rounded[1], False)
         quantize_wp(1, 0, 0, 4, rounded[1])
         early = held("early", [P, PACK * HALF], BF16)
@@ -340,10 +337,11 @@ def tile_list_importance_weighted_critic_kernel(
         weigh(1, HALF, UNIT, rounded[0], 1)
         quantize_z((0,), HALF, low[1])
         weave(high[0], high[1], 1)
-        weigh(0, HALF + UNIT, UNIT, low[2], 0)
+        weigh(0, HALF + UNIT, UNIT, low[2], 0, None, (0,))
         quantize_z((1,), HALF, high[1])
         for u in range(2):
             finish(4 + u, 2 * u, 2, 2, HALF, UNIT, 1)
+        weigh(0, HALF + UNIT, UNIT, low[2], 0, None, (1,))
         weave(low[2], low[0], 1)
         weigh(1, HALF + UNIT, P, eighth[0], 0)
         quantize_z((0,), HALF + UNIT, low[0], 2)

@@ -56,17 +56,21 @@ def tile_list_importance_weighted_critic_kernel(
         woven = held("woven", [P, 2 * PACK * HALF], BF16)
         ratio = {}
 
-        def hold_ratios(b, h, place=None):
-            both = held("ratio%d%d" % (b, h), [P, 2 * S], F32, place)
-            for u in range(2):
-                ratio[b, h, u] = both[:, u * S : (u + 1) * S]
+        def hold_ratios(b, j0, width, place=None):
+            both = held("ratio%d_%d" % (b, j0), [P, PACK * width], F32, place)
+            for j in range(j0, j0 + width, P):
+                ratio[b, j // P] = (both, j0, width)
 
         def ratios(b, u, j0, width):
-            first = 2 * (j0 % HALF)
-            return ratio[b, j0 // HALF, u][:, first : first + 2 * width]
+            both, start, span = ratio[b, j0 // P]
+            first = 2 * (u * span + j0 - start)
+            return both[:, first : first + 2 * width]
 
-        for b, h in ((0, 0), (0, 1), (1, 0)):
-            hold_ratios(b, h)
+        shared = held("shared", [P, 9 * PASS + UNIT], F32)
+        for j in range(0, S, P):
+            ratio[0, j // P] = (shared[:, j // HALF * 2 * S :], j // HALF * HALF, HALF)
+        hold_ratios(1, 0, HALF)
+        hold_ratios(1, HALF, UNIT)
         zq = {}
         wp_raw = {}
         adv_raw = {}
@@ -178,7 +182,7 @@ def tile_list_importance_weighted_critic_kernel(
                         columns, column_scales = g2w[:, cols], g2s[:, cols]
                     else:
                         weights, weight_scales = wpq[a, b, t][0].bitcast(FP8X4), wpq[a, b, t][1]
-                        columns, column_scales = g1w[a, j0 // UNIT][:, inner], g1s[4 + 4 * a : P, cols]
+                        columns, column_scales = g1w[a, j0 // UNIT][:, inner], g1s[j0 // HALF][4 + 4 * a : P, j0 % HALF : j0 % HALF + width]
                     nc.tensor.matmul_mx(
                         out=bank[:, e * width : (e + 1) * width],
                         lhsT=weights,
@@ -211,9 +215,11 @@ def tile_list_importance_weighted_critic_kernel(
                     ALU.mult,
                 )
 
-        def weave(buffer, grouped, blocks):
-            words = buffer.bitcast(I32).rearrange("p (b u j) -> p b j u", b=blocks, u=2)
-            nc.vector.tensor_copy(grouped.bitcast(I32).rearrange("p (b j u) -> p b j u", b=blocks, u=2), words)
+        def weave(buffer, grouped, on_vector=True):
+            word = I32 if on_vector else U32
+            move = nc.vector.tensor_copy if on_vector else nc.scalar.copy
+            words = buffer.bitcast(word).rearrange("p (u j) -> p j u", u=2)
+            move(grouped.bitcast(word).rearrange("p (j u) -> p j u", u=2), words)
 
         def quantize_z(blocks, j0, grouped, pieces=1):
             count = len(blocks) * pieces
@@ -266,12 +272,13 @@ def tile_list_importance_weighted_critic_kernel(
         load_words(v2_words, tab2_words[0])
         load_words(v_words[0], tab_words[0])
         load_planes(v_scales, tab_scales, 4, (1, 3), nc.gpsimd)
+        load_plane(wb_scales_raw, wb_scales, nc.sync)
         load_wp(0, 0, 1)
         load_planes(v_scales, tab_scales, 4, (0, 2), nc.sync)
-        load_plane(wb_scales_raw, wb_scales, nc.sync)
         load_wp(1, 0, 1)
-        load_wp(0, 1, 1)
         load_words(v_words[1], tab_words[1])
+        wp_raw[0, 1] = shared[:, PASS + UNIT :].rearrange("p (k c) -> p k c", k=PACK)[:, :, :PASS]
+        nc.sync.dma_start(out=wp_raw[0, 1], in_=wp[blk(0), blk(1)].rearrange("(p k) c -> p k c", k=PACK))
         load_wp(1, 1, 1)
         load_adv(0, 0, HALF)
         load_adv(1, 0, HALF)
@@ -289,38 +296,39 @@ def tile_list_importance_weighted_critic_kernel(
         for b in range(2):
             deal(wb_s[:, blk(b)], wb_scales_raw[:, blk(b)], nc.gpsimd.tensor_copy)
         gather_v(0, 0, [S])
-        round_wp(0, 0, 0, 4, rounded[0], False)
-        quantize_wp(0, 0, 0, 4, rounded[0])
-        g1s = gather("g1s", v_scales, list1, 0, S, U8)
+        g1s = [gather("g1s0", v_scales, list1, 0, HALF, U8)]
+        opening = held("opening", [P, PACK * HALF], BF16)
+        round_wp(0, 0, 0, 4, opening, False)
+        quantize_wp(0, 0, 0, 4, opening)
+        g1s.append(gather("g1s1", v_scales, list1, HALF, HALF, U8, "opening"))
         round_wp(1, 0, 0, 4, rounded[1], False)
         quantize_wp(1, 0, 0, 4, rounded[1])
-        early = held("early", [P, PACK * HALF], BF16)
-        round_wp(0, 1, 0, 4, early, False)
         gather_v(1, 0, [UNIT])
         gather_v(1, UNIT, [UNIT])
-        quantize_wp(0, 1, 0, 4, early)
-        gather_v(1, HALF, [HALF], "early")
-        for q in range(2):
+        gather_v(1, HALF, [HALF])
+        first_products(0, 0, 0, (0,))
+        round_wp(0, 1, 0, 2, rounded[2], False)
+        round_wp(0, 1, 2, 2, rounded[2], True)
+        quantize_wp(0, 1, 0, 4, rounded[2])
+        first_products(0, 0, 0, (1,))
+        for q in range(1, 4):
             first_products(0, q, 2 * q)
         round_wp(1, 1, 0, 4, rounded[0], True)
         quantize_wp(1, 1, 0, 4, rounded[0])
-        for q in range(2):
-            first_products(1, q, 4 + 2 * q)
-        for q in range(2, 4):
-            first_products(0, q, 2 * (q - 2))
+        for q in range(3):
+            first_products(1, q, 2 * (q % 2))
         half = [slice(b * PACK * HALF, (b + 1) * PACK * HALF) for b in range(2)]
         weigh(0, 0, HALF, pairs, 0)
-        weave(pairs[:, half[0]], woven[:, half[0]], 1)
+        weave(pairs[:, half[0]], woven[:, half[0]])
         weigh(1, 0, HALF, pairs, 1)
         quantize_z((0,), 0, woven[:, half[0]])
-        weave(pairs[:, half[1]], woven[:, half[1]], 1)
+        weave(pairs[:, half[1]], woven[:, half[1]])
         spent = {}
         for b in range(2):
             for u in range(2):
                 spent[b, u] = ratios(b, u, 0, UNIT).bitcast(BF16)
                 round_wc(b, 2 * u, 2, spent[b, u], False)
-        hold_ratios(1, 1, "wc1")
-        first_products(1, 2, 4)
+        hold_ratios(1, HALF + UNIT, UNIT, "wc1")
         quantize_z((1,), 0, woven[:, half[1]])
         for u in range(2):
             quantize_wc(0, 2 * u, 2, spent[0, u])
@@ -330,25 +338,24 @@ def tile_list_importance_weighted_critic_kernel(
         for u in range(2):
             quantize_wc(1, 2 * u, 2, spent[1, u])
         for n in range(4):
-            finish(n, n, 1, 1, 0, HALF, 1)
-        first_products(1, 3, 6)
+            finish(4 + n, n, 1, 1, 0, HALF, 1)
+        first_products(1, 3, 2)
         weigh(0, HALF, UNIT, rounded[0], 0)
-        weave(low[0], low[1], 1)
+        weave(low[0], low[1])
         weigh(1, HALF, UNIT, rounded[0], 1)
         quantize_z((0,), HALF, low[1])
-        weave(high[0], high[1], 1)
-        weigh(0, HALF + UNIT, UNIT, low[2], 0, None, (0,))
+        weave(high[0], high[1])
+        weigh(0, HALF + UNIT, UNIT, low[2], 0)
         quantize_z((1,), HALF, high[1])
         for u in range(2):
-            finish(4 + u, 2 * u, 2, 2, HALF, UNIT, 1)
-        weigh(0, HALF + UNIT, UNIT, low[2], 0, None, (1,))
-        weave(low[2], low[0], 1)
+            finish(u, 2 * u, 2, 2, HALF, UNIT, 1)
+        weave(low[2], low[0])
         weigh(1, HALF + UNIT, P, eighth[0], 0)
         quantize_z((0,), HALF + UNIT, low[0], 2)
-        weave(eighth[0], pairs[:, :PASS], 1)
+        weave(eighth[0], pairs[:, :PASS])
         weigh(1, HALF + UNIT + P, P, eighth[1], 0)
         quantize_z((1,), HALF + UNIT, pairs[:, :PASS])
-        weave(eighth[1], woven[:, :PASS], 1)
+        weave(eighth[1], woven[:, :PASS])
         quantize_z((1,), HALF + UNIT + P, woven[:, :PASS])
         for g in range(2):
-            finish(6 + 2 * g, 0, 4, 2, HALF + UNIT + g * P, P, 1)
+            finish(2 + 2 * g, 0, 4, 2, HALF + UNIT + g * P, P, 1)

@@ -270,9 +270,9 @@ def tile_list_importance_weighted_critic_kernel(
         nc.sync.dma_start(out=wb_raw[:].bitcast(I32), in_=wb_words[0].bitcast(I32))
         load_plane(v2_scales, tab2_scales, nc.sync)
         load_words(v2_words, tab2_words[0])
-        load_words(v_words[0], tab_words[0])
         load_planes(v_scales, tab_scales, 4, (1, 3), nc.gpsimd)
         load_plane(wb_scales_raw, wb_scales, nc.sync)
+        load_words(v_words[0], tab_words[0])
         load_wp(0, 0, 1)
         load_planes(v_scales, tab_scales, 4, (0, 2), nc.sync)
         load_wp(1, 0, 1)
@@ -293,8 +293,7 @@ def tile_list_importance_weighted_critic_kernel(
         deal(wb_q[:].bitcast(U16), wb_raw[:].bitcast(U16), nc.scalar.copy)
         g2s = gather("g2s", v2_scales, list2, 0, S, U8)
         g2w = gather("g2w", v2_words, list2, 0, S, U32, "v2_scales")
-        for b in range(2):
-            deal(wb_s[:, blk(b)], wb_scales_raw[:, blk(b)], nc.gpsimd.tensor_copy)
+        deal(wb_s[:], wb_scales_raw[:], nc.vector.tensor_copy)
         gather_v(0, 0, [S])
         g1s = [gather("g1s0", v_scales, list1, 0, HALF, U8)]
         opening = held("opening", [P, PACK * HALF], BF16)

@@ -282,10 +282,10 @@ def tile_list_importance_weighted_critic_kernel(
         load_wp(1, 1, 1)
         load_adv(0, 0, HALF)
         load_adv(1, 0, HALF)
-        load_bias()
         load_wc(0)
         load_wc(1)
         load_adv(0, HALF, UNIT)
+        load_bias()
         load_adv(1, HALF, UNIT)
         load_adv(0, HALF + UNIT, UNIT)
         load_adv(1, HALF + UNIT, UNIT)

from contextlib import ExitStack

import concourse.mybir as mybir

K, K2, T, S, H, N = 1024, 512, 2048, 1024, 1024, 512
FLOPS = 2 * S * (K * H + K2 * H + H * N)

F32 = mybir.dt.float32
BF16 = mybir.dt.bfloat16
I32 = mybir.dt.int32
U32 = mybir.dt.uint32
U16 = mybir.dt.uint16
U8 = mybir.dt.uint8
FP8X4 = mybir.dt.float8_e4m3fn_x4
FP4X4 = mybir.dt.float4_e2m1fn_x4
ACT = mybir.ActivationFunctionType
ALU = mybir.AluOpType

P = 128
PACK = 4
PASS = P * PACK
HALF = 512
UNIT = 256
CLIP = 2.0
WB = 2


def tile_list_importance_weighted_critic_kernel(
    tc, tab_words, tab_scales, tab2_words, tab2_scales, offs, offs2, wp, wb_words, wb_scales, adv, wc, bc, out
):
    nc = tc.nc
    with ExitStack() as ctx:
        keep = ctx.enter_context(tc.tile_pool(name="keep", bufs=1))
        psum = ctx.enter_context(tc.psum_pool(name="psum", bufs=1))

        def held(name, shape, dtype, place=None):
            return keep.tile(shape, dtype, name=name, tag=place or name, align_bytes=64)

        def blk(i):
            return slice(i * PASS, (i + 1) * PASS)

        list1 = held("list1", [P, S // 16], U16)
        list2 = held("list2", [P, S // 16], U16)
        v_words = [held("v_words%d" % a, [P, T], U32) for a in range(2)]
        v2_words = held("v2_words", [P, T], U32)
        v_scales = held("v_scales", [P, T], U8)
        v2_scales = held("v2_scales", [P, T], U8)
        wb_raw = held("wb_raw", [P, 2 * H], U8)
        wb_scales_raw = held("wb_scales_raw", [P, H], U8)
        wb_q = held("wb_q", [P, 2 * H], U8)
        wb_s = held("wb_s", [P, H], U8)
        bias = held("bias", [P, N // P], F32)
        banks = [psum.tile([P, HALF], F32, name="bank%d" % i) for i in range(8)]
        rounded = [held("rounded%d" % i, [P, PACK * HALF], BF16) for i in range(3)]
        pairs = held("pairs", [P, 2 * PACK * HALF], BF16)
        woven = held("woven", [P, 2 * PACK * HALF], BF16)
        ratio = {}

        def hold_ratios(b, j0, width, place=None):
            both = held("ratio%d_%d" % (b, j0), [P, PACK * width], F32, place)
            for j in range(j0, j0 + width, P):
                ratio[b, j // P] = (both, j0, width)

        def ratios(b, u, j0, width):
            both, start, span = ratio[b, j0 // P]
            first = 2 * (u * span + j0 - start)
            return both[:, first : first + 2 * width]

        shared = held("shared", [P, 9 * PASS + UNIT], F32)
        for j in range(0, S, P):
            ratio[0, j // P] = (shared[:, j // HALF * 2 * S :], j // HALF * HALF, HALF)
        hold_ratios(1, 0, HALF)
        hold_ratios(1, HALF, UNIT)
        zq = {}
        wp_raw = {}
        adv_raw = {}
        wc_raw = {}
        wpq = {}
        wcq = {}
        g1w = {}

        def load_words(dst, src):
            nc.sync.dma_start(out=dst[:].bitcast(I32), in_=src.rearrange("p t i -> p (t i)").bitcast(I32))

        def load_planes(dst, src, first, quadrants, queue):
            for q in quadrants:
                queue.dma_start(
                    out=dst[32 * q + first : 32 * q + first + 8, :].bitcast(I32),
                    in_=src[:, 4 * q : 4 * q + 4, :].bitcast(I32),
                )

        def load_plane(dst, src, queue):
            for r in range(4):
                queue.dma_start(out=dst[r:P:32, :].bitcast(I32), in_=src[0, r:16:4, :].bitcast(I32))

        def load_rows(name, src):
            raw = held(name, [P, PACK, src.shape[1]], F32)
            nc.sync.dma_start(out=raw[:], in_=src.rearrange("(p k) c -> p k c", k=PACK))
            return raw

        def load_wp(a, b0, count):
            raw = load_rows("wp%d%d" % (a, b0), wp[blk(a), b0 * PASS : (b0 + count) * PASS])
            for b in range(count):
                wp_raw[a, b0 + b] = raw[:, :, blk(b)]

        def load_adv(b, j0, width):
            raw = load_rows("adv%d_%d" % (b, j0), adv[blk(b), j0 : j0 + width])
            for j in range(j0, j0 + width, P):
                adv_raw[b, j // P] = (raw, j0)

        def load_wc(b):
            wc_raw[b] = load_rows("wc%d" % b, wc[blk(b), :])

        def load_bias():
            with nc.allow_non_contiguous_dma(reason="one bias value a partition"):
                nc.sync.dma_start(out=bias[:], in_=bc.rearrange("(c p) -> p c", p=P))

        def gather(name, window, offsets, j0, width, dtype, place=None):
            picked = held(name, [P, width], dtype, place)
            nc.vector.tensor_copy(picked[:], window[:].indirect(offsets[:, j0 // 16 : (j0 + width) // 16]))
            return picked

        def gather_v(a, j0, widths, place=None):
            picked = held("g1w%d_%d" % (a, j0), [P, sum(widths)], U32, place)
            first = 0
            for width in widths:
                offsets = list1[:, (j0 + first) // 16 : (j0 + first + width) // 16]
                nc.vector.tensor_copy(picked[:, first : first + width], v_words[a][:].indirect(offsets))
                first = first + width
            for j in range(0, first, UNIT):
                g1w[a, (j0 + j) // UNIT] = picked[:, j : j + UNIT]

        def deal(dst, src, move):
            blocks = src.shape[1] // PASS
            move(
                dst.rearrange("p (b t m) -> p b t m", b=blocks, t=PACK),
                src.rearrange("p (b m t) -> p b t m", b=blocks, t=PACK),
            )

        def quantize(name, grouped):
            width = grouped.shape[1] // PACK
            codes = held(name + "_codes", [P, width], U32)
            scales = held(name + "_scales", [P, width], U8)
            nc.vector.quantize_mx(out=codes[:].bitcast(FP8X4), scales=scales[:], in_=grouped)
            return [(codes[:, c : c + P], scales[:, c : c + P]) for c in range(0, width, P)]

        def round_wp(a, b, t0, count, buffer, on_vector):
            grouped = buffer[:, t0 * PASS : (t0 + count) * PASS]
            dst = grouped.rearrange("p (t m k) -> p m k t", t=count, k=PACK)
            src = wp_raw[a, b].rearrange("p k (m t) -> p m k t", t=PACK)[:, :, :, t0 : t0 + count]
            if on_vector:
                nc.vector.tensor_scalar(dst, src, -1.0, None, ALU.mult)
            else:
                nc.scalar.activation(dst, src, ACT.Copy, scale=-1.0)

        def quantize_wp(a, b, t0, count, buffer):
            grouped = buffer[:, t0 * PASS : (t0 + count) * PASS]
            for t, operand in enumerate(quantize("wp%d%d%d" % (a, b, t0), grouped)):
                wpq[a, b, t0 + t] = operand

        def round_wc(b, n0, count, grouped, on_vector):
            dst = grouped.rearrange("p (c i k) -> p c k i", i=4, k=PACK)
            src = wc_raw[b][:, :, n0 * P : (n0 + count) * P].rearrange("p k (c i) -> p c k i", i=4)
            if on_vector:
                nc.vector.tensor_copy(dst, src)
            else:
                nc.scalar.activation(dst, src, ACT.Copy)

        def quantize_wc(b, n0, count, grouped):
            for n, operand in enumerate(quantize("wc%d%d" % (b, n0), grouped)):
                wcq[b, n0 + n] = operand

        def products(b, t0, slots, j0, width, bank, passes=(WB, 0, 1)):
            cols = slice(j0, j0 + width)
            inner = slice(j0 % UNIT, j0 % UNIT + width)
            for a in passes:
                for e in range(slots):
                    t = t0 + e
                    if a == WB:
                        c0 = b * PASS + t * P
                        weights, weight_scales = wb_q[:, 2 * c0 : 2 * (c0 + P)].bitcast(FP4X4), wb_s[:, c0 : c0 + P]
                        columns, column_scales = g2w[:, cols], g2s[:, cols]
                    else:
                        weights, weight_scales = wpq[a, b, t][0].bitcast(FP8X4), wpq[a, b, t][1]
                        columns, column_scales = g1w[a, j0 // UNIT][:, inner], g1s[j0 // HALF][4 + 4 * a : P, j0 % HALF : j0 % HALF + width]
                    nc.tensor.matmul_mx(
                        out=bank[:, e * width : (e + 1) * width],
                        lhsT=weights,
                        lhsT_scale=weight_scales,
                        rhs=columns.bitcast(FP8X4),
                        rhs_scale=column_scales,
                        start=(a == WB and e == 0),
                        stop=(a == 1 and e == slots - 1),
                    )

        def exponential(target, bank, slots):
            woven_ratios = target.rearrange("p (j e) -> p j e", e=slots)
            nc.scalar.activation(woven_ratios, bank[:].rearrange("p (e j) -> p j e", e=slots), ACT.Exp, scale=-1.0)

        def first_products(b, q, first_bank, halves=(0, 1), passes=(WB, 0, 1)):
            for u in halves:
                products(b, 2 * u, 2, q * UNIT, UNIT, banks[first_bank + u], passes)
                exponential(ratios(b, u, q * UNIT, UNIT), banks[first_bank + u], 2)

        def weigh(b, j0, width, buffer, place, span=None, slot_pairs=(0, 1)):
            raw, start = adv_raw[b, j0 // P]
            for u in slot_pairs:
                first = 2 * ((2 * place + u) * (span or width) + j0 % (span or width))
                nc.vector.scalar_tensor_tensor(
                    buffer[:, first : first + 2 * width].rearrange("p (j e) -> p j e", e=2),
                    ratios(b, u, j0, width).rearrange("p (j e) -> p j e", e=2),
                    CLIP,
                    raw[:, 2 * u : 2 * u + 2, j0 - start : j0 - start + width].rearrange("p e j -> p j e"),
                    ALU.min,
                    ALU.mult,
                )

        def weave(buffer, grouped, on_vector=True):
            word = I32 if on_vector else U32
            move = nc.vector.tensor_copy if on_vector else nc.scalar.copy
            words = buffer.bitcast(word).rearrange("p (u j) -> p j u", u=2)
            move(grouped.bitcast(word).rearrange("p (j u) -> p j u", u=2), words)

        def quantize_z(blocks, j0, grouped, pieces=1):
            count = len(blocks) * pieces
            width = grouped.shape[1] // (count * PACK)
            codes = held("z_codes%d_%d" % (blocks[0], j0), [P, count * width], U32)
            scales = held("z_scales%d_%d" % (blocks[0], j0), [P, count * width], U8)
            nc.vector.quantize_mx(out=codes[:].bitcast(FP8X4), scales=scales[:], in_=grouped)
            for i in range(count):
                cols = slice(i * width, (i + 1) * width)
                zq[blocks[i // pieces], j0 + i % pieces * width] = (codes[:, cols], scales[:, cols])

        def critic(bank, result, n0, count, j0, width, on_vector):
            for b in range(2):
                for e in range(count):
                    codes, scales = wcq[b, n0 + e]
                    nc.tensor.matmul_mx(
                        out=bank[:, e * width : (e + 1) * width],
                        lhsT=codes.bitcast(FP8X4),
                        lhsT_scale=scales,
                        rhs=zq[b, j0][0].bitcast(FP8X4),
                        rhs_scale=zq[b, j0][1],
                        start=(b == 0 and e == 0),
                        stop=(b == 1 and e == count - 1),
                    )
            if on_vector:
                sums = bank[:, : count * width].rearrange("p (e j) -> p e j", e=count)
                spread = bias[:, n0 : n0 + count].unsqueeze(2).to_broadcast([P, count, width])
                nc.vector.tensor_tensor(result, sums, spread, ALU.add)
            else:
                for e in range(count):
                    source = bank[:, e * width : (e + 1) * width]
                    nc.scalar.activation(result[:, e, :], source, ACT.Identity, bias=bias[:, n0 + e : n0 + e + 1])

        def finish(first_bank, n0, tiles, count, j0, width, vector_from, queue=nc.sync):
            result = held("result%d_%d" % (j0, n0), [P, tiles, width], F32)
            for i, n in enumerate(range(0, tiles, count)):
                bank = banks[(first_bank + i) % 8]
                critic(bank, result[:, n : n + count, :], n0 + n, count, j0, width, i >= vector_from)
            rows = out[n0 * P : (n0 + tiles) * P, j0 : j0 + width]
            queue.dma_start(out=rows.rearrange("(e p) j -> p e j", p=P), in_=result[:])

        nc.gpsimd.memset(v2_scales[:].bitcast(I32), 0)
        nc.vector.memset(v_scales[:].bitcast(I32), 0)
        nc.vector.memset(wb_scales_raw[:].bitcast(I32), 0)

        nc.sync.dma_start(list2[:], offs2)
        nc.sync.dma_start(list1[:], offs)
        nc.sync.dma_start(out=wb_raw[:].bitcast(I32), in_=wb_words[0].bitcast(I32))
        load_plane(v2_scales, tab2_scales, nc.sync)
        load_words(v2_words, tab2_words[0])
        load_planes(v_scales, tab_scales, 4, (1, 3), nc.gpsimd)
        load_plane(wb_scales_raw, wb_scales, nc.sync)
        load_words(v_words[0], tab_words[0])
        load_wp(0, 0, 1)
        load_planes(v_scales, tab_scales, 4, (0, 2), nc.sync)
        load_wp(1, 0, 1)
        load_words(v_words[1], tab_words[1])
        wp_raw[0, 1] = shared[:, PASS + UNIT :].rearrange("p (k c) -> p k c", k=PACK)[:, :, :PASS]
        nc.sync.dma_start(out=wp_raw[0, 1], in_=wp[blk(0), blk(1)].rearrange("(p k) c -> p k c", k=PACK))
        load_wp(1, 1, 1)
        load_adv(0, 0, HALF)
        load_adv(1, 0, HALF)
        load_wc(0)
        load_wc(1)
        load_adv(0, HALF, UNIT)
        load_bias()
        load_adv(1, HALF, UNIT)
        load_adv(0, HALF + UNIT, UNIT)
        load_adv(1, HALF + UNIT, UNIT)

        deal(wb_q[:].bitcast(U16), wb_raw[:].bitcast(U16), nc.scalar.copy)
        g2s = gather("g2s", v2_scales, list2, 0, S, U8)
        g2w = gather("g2w", v2_words, list2, 0, S, U32, "v2_scales")
        deal(wb_s[:], wb_scales_raw[:], nc.vector.tensor_copy)
        gather_v(0, 0, [S])
        g1s = [gather("g1s0", v_scales, list1, 0, HALF, U8)]
        opening = held("opening", [P, PACK * HALF], BF16)
        round_wp(0, 0, 0, 4, opening, False)
        quantize_wp(0, 0, 0, 4, opening)
        g1s.append(gather("g1s1", v_scales, list1, HALF, HALF, U8, "opening"))
        round_wp(1, 0, 0, 4, rounded[1], False)
        quantize_wp(1, 0, 0, 4, rounded[1])
        gather_v(1, 0, [UNIT])
        gather_v(1, UNIT, [UNIT])
        gather_v(1, HALF, [HALF])
        first_products(0, 0, 0, (0,))
        round_wp(0, 1, 0, 2, rounded[2], False)
        round_wp(0, 1, 2, 2, rounded[2], True)
        quantize_wp(0, 1, 0, 4, rounded[2])
        first_products(0, 0, 0, (1,))
        for q in range(1, 4):
            first_products(0, q, 2 * q)
        round_wp(1, 1, 0, 4, rounded[0], True)
        quantize_wp(1, 1, 0, 4, rounded[0])
        for q in range(3):
            first_products(1, q, 2 * (q % 2))
        half = [slice(b * PACK * HALF, (b + 1) * PACK * HALF) for b in range(2)]
        weigh(0, 0, HALF, pairs, 0)
        weave(pairs[:, half[0]], woven[:, half[0]])
        weigh(1, 0, HALF, pairs, 1)
        quantize_z((0,), 0, woven[:, half[0]])
        weave(pairs[:, half[1]], woven[:, half[1]])
        spent = {}
        for b in range(2):
            for u in range(2):
                spent[b, u] = ratios(b, u, 0, UNIT).bitcast(BF16)
                round_wc(b, 2 * u, 2, spent[b, u], False)
        hold_ratios(1, HALF + UNIT, UNIT, "wc1")
        quantize_z((1,), 0, woven[:, half[1]])
        for u in range(2):
            quantize_wc(0, 2 * u, 2, spent[0, u])
        low = [buffer[:, : 2 * PASS] for buffer in rounded]
        high = [buffer[:, 2 * PASS :] for buffer in rounded]
        eighth = [rounded[2][:, (2 + g) * PASS : (3 + g) * PASS] for g in range(2)]
        for u in range(2):
            quantize_wc(1, 2 * u, 2, spent[1, u])
        for n in range(4):
            finish(4 + n, n, 1, 1, 0, HALF, 1)
        first_products(1, 3, 2)
        weigh(0, HALF, UNIT, rounded[0], 0)
        weave(low[0], low[1])
        weigh(1, HALF, UNIT, rounded[0], 1)
        quantize_z((0,), HALF, low[1])
        weave(high[0], high[1])
        weigh(0, HALF + UNIT, UNIT, low[2], 0)
        quantize_z((1,), HALF, high[1])
        for u in range(2):
            finish(u, 2 * u, 2, 2, HALF, UNIT, 1)
        weave(low[2], low[0])
        weigh(1, HALF + UNIT, P, eighth[0], 0)
        quantize_z((0,), HALF + UNIT, low[0], 2)
        weave(eighth[0], pairs[:, :PASS])
        weigh(1, HALF + UNIT + P, P, eighth[1], 0)
        quantize_z((1,), HALF + UNIT, pairs[:, :PASS])
        weave(eighth[1], woven[:, :PASS])
        quantize_z((1,), HALF + UNIT + P, woven[:, :PASS])
        for g in range(2):
            finish(2 + 2 * g, 0, 4, 2, HALF + UNIT + g * P, P, 1)
